import numpy as np
import ml_dtypes


def mxq(x, axis, fmt="e4m3"):
    dtype, down = {"e4m3": (ml_dtypes.float8_e4m3fn, 7), "e5m2": (ml_dtypes.float8_e5m2, 14)}[fmt]
    v = np.moveaxis(np.asarray(x, np.float32).astype(ml_dtypes.bfloat16).astype(np.float64), axis, -1)
    blocks = v.reshape(v.shape[:-1] + (-1, 32))
    amax = np.abs(blocks).max(-1, keepdims=True)
    byte = np.maximum(np.where(amax > 0, np.frexp(amax)[1] - 1 + 127, 0) - down, 1)
    scale = np.exp2(byte - 127.0)
    codes = (blocks / scale).astype(np.float32).astype(dtype).astype(np.float64)
    return np.moveaxis((codes * scale).reshape(v.shape), -1, axis)


WIDE = False


def mx_kscale(k):
    if not WIDE:
        return np.ones(k)
    levels = np.array([10, -10, 5, -5, 0])
    if k % 512:
        return np.exp2(np.random.permutation(np.resize(levels, k // 32))).repeat(32)
    a = np.empty((k // 512, 16))
    for p in range(k // 512):
        a[p, :8] = np.random.permutation(np.resize(levels, 8))
        for g in range(8):
            far = levels[np.abs(levels - a[p, g]) >= 10]
            a[p, g + 8] = far[np.random.randint(len(far))]
    return np.exp2(a.ravel()).repeat(32)


def f64(x):
    return np.asarray(x).astype(np.float64)


def striped(idx):
    return np.tile(idx.reshape(-1, 16).T, (8, 1)).astype(np.uint16)


def unstriped(offs):
    return offs[:16].T.reshape(-1).astype(np.int64)


def pack_weight(w):
    k, n = w.shape
    w = f64(np.asarray(w, np.float32).astype(ml_dtypes.bfloat16)).reshape(k // 32, 32, n)
    amax = np.abs(w).max(1)
    byte = np.clip(np.where(amax > 0, np.frexp(amax)[1] - 1 + 127 - 7, 1), 1, 254)
    scaled = (w * np.exp2(127.0 - byte)[:, None, :]).reshape(k, n).astype(np.float32)
    words = np.ascontiguousarray(scaled.reshape(k // 512, 128, 4, n).transpose(0, 1, 3, 2)).astype(ml_dtypes.float8_e4m3fn).view(np.uint8)
    return words, np.ascontiguousarray(byte.astype(np.uint8).reshape(k // 512, 16, n))


def unpack_weight(words, scales):
    g, p, n, _ = words.shape
    vals = np.ascontiguousarray(words).view(ml_dtypes.float8_e4m3fn).astype(np.float64) * np.repeat(np.exp2(scales.astype(np.float64) - 127.0), 8, axis=1)[..., None]
    return vals.transpose(0, 1, 3, 2).reshape(g * 512, n)


def sigmoid(v):
    return 1.0 / (1.0 + np.exp(-np.maximum(v, -700.0)))


K, T, S, H, N = 512, 2048, 1024, 1024, 128


def setup_inputs():
    n = np.random.standard_normal
    s = mx_kscale(K)[:, None]
    u = mx_kscale(H)
    packed = pack_weight(n((K, T)) * s)
    return {
        "x_words": packed[0],
        "x_scales": packed[1],
        "w1": (n((K, H)) / np.sqrt(K) / s).astype(np.float32),
        "w3": (n((K, H)) / np.sqrt(K) / s * u).astype(np.float32),
        "w2": (n((H, N)) / np.sqrt(H) / u[:, None]).astype(np.float32),
        "gate": np.tile(np.random.uniform(0.2, 1.0, S), (N, 1)).astype(np.float32),
        "offs": striped(np.sort(np.random.permutation(T)[:S])),
    }


def reference(x_words, x_scales, w1, w3, w2, gate, offs):
    idx = unstriped(offs)
    xq = unpack_weight(x_words, x_scales)[:, idx]
    h = sigmoid(mxq(f64(w1), 0, "e4m3").T @ xq) * (mxq(f64(w3), 0, "e4m3").T @ xq)
    y = mxq(f64(w2), 0, "e4m3").T @ mxq(h, 0, "e4m3")
    out = np.zeros((N, T))
    out[:, idx] = f64(gate) * y
    return out

@@ -1,0 +1,224 @@
+from contextlib import ExitStack
+
+import concourse.mybir as mybir
+
+K, T, S, H, N = 512, 2048, 1024, 1024, 128
+FLOPS = 2 * S * (2 * K * H + H * N)
+
+F32 = mybir.dt.float32
+BF16 = mybir.dt.bfloat16
+I32 = mybir.dt.int32
+U32 = mybir.dt.uint32
+U16 = mybir.dt.uint16
+U8 = mybir.dt.uint8
+FP8X4 = mybir.dt.float8_e4m3fn_x4
+MULT = mybir.AluOpType.mult
+SIGMOID = mybir.ActivationFunctionType.Sigmoid
+
+P = 128
+PACK = 4
+PASS = P * PACK
+TOK = 128
+CHUNK = 256
+
+
+def tile_picked_depth_glu_sigmoid_srt_p_kernel(
+    tc, x_words, x_scales, w1, w3, w2, gate, offs, out
+):
+    nc = tc.nc
+    with ExitStack() as ctx:
+        lists = ctx.enter_context(tc.tile_pool(name="lists", bufs=1))
+        keep = ctx.enter_context(tc.tile_pool(name="keep", bufs=1))
+        psum = ctx.enter_context(tc.psum_pool(name="psum", bufs=1))
+
+        def sb(shape, dtype, name):
+            return keep.tile(shape, dtype, name=name, align_bytes=64)
+
+        offsets = lists.tile([P, S // 16], U16, name="offsets")
+
+        def entries(lo, hi):
+            return offsets[:, lo // 16 : hi // 16]
+
+        scale_window = sb([P, T // 4], I32, "scale_window")
+        nc.vector.memset(scale_window[:], 0)
+        result = sb([P, T], F32, "result")
+        nc.vector.memset(result[:], 0.0)
+        warm = sb([P, 2], F32, "warm")
+        nc.vector.memset(warm[:, 0:1], 0.0)
+
+        nc.scalar.activation(out=warm[:, 1:2], in_=warm[:, 0:1], func=SIGMOID)
+
+        raw = {}
+
+        def load_first_layer(name, w, g):
+            raw[name, g] = sb([P, PACK, PASS], F32, "raw_%s_%d" % (name, g))
+            nc.sync.dma_start(
+                out=raw[name, g][:],
+                in_=w.rearrange("(p j) c -> p j c", j=PACK)[:, :, g * PASS : (g + 1) * PASS],
+            )
+
+        nc.sync.dma_start(offsets[:], offs)
+        load_first_layer("w1", w1, 0)
+        scale_rows = x_scales[0].bitcast(I32)
+        for q in range(4):
+            nc.sync.dma_start(out=scale_window[32 * q : 32 * q + 4, :], in_=scale_rows[4 * q : 4 * q + 4, :])
+        word_window = sb([P, T], U32, "word_window")
+        nc.sync.dma_start(
+            out=word_window[:].bitcast(I32), in_=x_words[0].rearrange("p n t -> p (n t)").bitcast(I32)
+        )
+        load_first_layer("w3", w3, 0)
+        load_first_layer("w1", w1, 1)
+        load_first_layer("w3", w3, 1)
+        raw_w2 = sb([P, 2, PACK, N], F32, "raw_w2")
+        nc.sync.dma_start(out=raw_w2[:], in_=w2.rearrange("(g p j) n -> p g j n", g=2, j=PACK))
+        gates = sb([P, S], F32, "gates")
+        nc.sync.dma_start(out=gates[:], in_=gate)
+
+        grouped, codes, scales = {}, {}, {}
+        for name in ("w1", "w3"):
+            for g in range(2):
+                grouped[name, g] = sb([P, PACK, P, PACK], BF16, "grouped_%s_%d" % (name, g))
+                codes[name, g] = sb([P, PASS], U32, "codes_%s_%d" % (name, g))
+                scales[name, g] = sb([P, PASS], U8, "scales_%s_%d" % (name, g))
+
+        def cast(copy, name, g, m_lo, m_hi):
+            copy(
+                out=grouped[name, g][:, :, m_lo:m_hi, :].rearrange("p t m j -> p m j t"),
+                in_=raw[name, g][:, :, PACK * m_lo : PACK * m_hi].rearrange("p j (m t) -> p m j t", t=PACK),
+            )
+
+        def quantise_weights(name, g, t_lo, t_hi):
+            cols = slice(t_lo * P, t_hi * P)
+            nc.vector.quantize_mx(
+                out=codes[name, g][:, cols].bitcast(FP8X4),
+                scales=scales[name, g][:, cols],
+                in_=grouped[name, g][:, t_lo:t_hi].rearrange("p t m j -> p (t m j)"),
+            )
+
+        x_codes = sb([P, S], U32, "x_codes")
+        x_bytes = sb([P, S], U8, "x_bytes")
+
+        def gather_words(lo, hi):
+            nc.vector.tensor_copy(x_codes[:, lo:hi], word_window[:].indirect(entries(lo, hi)))
+
+        def first_layer(name, g, n, bufs):
+            bank = psum.tile([P, PACK, TOK], F32, name="bank_" + name, tag="bank_" + name, bufs=bufs)
+            toks = slice(n * TOK, (n + 1) * TOK)
+            for t in range(PACK):
+                cols = slice(t * P, (t + 1) * P)
+                nc.tensor.matmul_mx(
+                    out=bank[:, t, :],
+                    lhsT=codes[name, g][:, cols].bitcast(FP8X4),
+                    lhsT_scale=scales[name, g][:, cols],
+                    rhs=x_codes[:, toks].bitcast(FP8X4),
+                    rhs_scale=x_bytes[:, toks],
+                    start=True,
+                    stop=True,
+                )
+            return bank
+
+        sig = {}
+
+        def sigmoid_tile(g, n):
+            bank = first_layer("w1", g, n, 3)
+            sig[g, n] = sb([P, TOK, PACK], F32, "sig_%d_%d" % (g, n))
+            nc.scalar.activation(out=sig[g, n][:], in_=bank[:].rearrange("p t n -> p n t"), func=SIGMOID)
+
+        hidden = [sb([P, S, PACK], BF16, "hidden_%d" % g) for g in range(2)]
+        h_codes = [sb([P, S], U32, "h_codes_%d" % g) for g in range(2)]
+        h_scales = [sb([P, S], U8, "h_scales_%d" % g) for g in range(2)]
+
+        def gated_tile(g, n):
+            bank = first_layer("w3", g, n, 3)
+            nc.vector.tensor_tensor(
+                out=hidden[g][:, n * TOK : (n + 1) * TOK, :],
+                in0=bank[:].rearrange("p t n -> p n t"),
+                in1=sig[g, n][:],
+                op=MULT,
+            )
+
+        def quantise_hidden(g, lo, hi):
+            nc.vector.quantize_mx(
+                out=h_codes[g][:, lo:hi].bitcast(FP8X4),
+                scales=h_scales[g][:, lo:hi],
+                in_=hidden[g][:, lo:hi, :].rearrange("p n t -> p (n t)"),
+            )
+
+        grouped_w2 = sb([P, 2, N, PACK], BF16, "grouped_w2")
+        w2_codes = sb([P, 2 * N], U32, "w2_codes")
+        w2_scales = sb([P, 2 * N], U8, "w2_scales")
+        y = sb([P, S], F32, "y")
+
+        def second_layer(c):
+            toks = slice(c * CHUNK, (c + 1) * CHUNK)
+            bank = psum.tile([P, CHUNK], F32, name="bank_y", tag="bank_y", bufs=2)
+            for g in range(2):
+                cols = slice(g * N, (g + 1) * N)
+                nc.tensor.matmul_mx(
+                    out=bank[:],
+                    lhsT=w2_codes[:, cols].bitcast(FP8X4),
+                    lhsT_scale=w2_scales[:, cols],
+                    rhs=h_codes[g][:, toks].bitcast(FP8X4),
+                    rhs_scale=h_scales[g][:, toks],
+                    start=(g == 0),
+                    stop=(g == 1),
+                )
+            nc.scalar.copy(out=y[:, toks], in_=bank[:])
+
+        def scatter(c):
+            lo, hi = c * CHUNK, (c + 1) * CHUNK
+            nc.vector.tensor_tensor(result[:].indirect(entries(lo, hi)), y[:, lo:hi], gates[:, lo:hi], MULT)
+
+        nc.vector.tensor_copy(x_bytes[:], scale_window[:].bitcast(U8).indirect(offsets[:]))
+        cast(nc.vector.tensor_copy, "w1", 0, 0, P)
+        quantise_weights("w1", 0, 0, PACK)
+        gather_words(0, 256)
+        gather_words(256, 512)
+        gather_words(512, 1024)
+        sigmoid_tile(0, 0)
+        sigmoid_tile(0, 1)
+        cast(nc.vector.tensor_copy, "w3", 0, 0, 84)
+        cast(nc.scalar.copy, "w3", 0, 84, P)
+        quantise_weights("w3", 0, 0, 2)
+        quantise_weights("w3", 0, 2, 4)
+        for n in range(2, 8):
+            sigmoid_tile(0, n)
+        cast(nc.scalar.copy, "w1", 1, 0, P)
+        for n in range(5):
+            gated_tile(0, n)
+        quantise_hidden(0, 0, 512)
+        for n in range(5, 8):
+            gated_tile(0, n)
+        quantise_weights("w1", 1, 0, PACK)
+        cast(nc.scalar.copy, "w3", 1, 32, P)
+        cast(nc.vector.tensor_copy, "w3", 1, 0, 32)
+        quantise_hidden(0, 512, 1024)
+        sigmoid_tile(1, 0)
+        sigmoid_tile(1, 1)
+        quantise_weights("w3", 1, 0, 2)
+        quantise_weights("w3", 1, 2, 4)
+        nc.scalar.copy(
+            out=grouped_w2[:].rearrange("p g (c i) j -> p g c j i", i=4),
+            in_=raw_w2[:].rearrange("p g j (c i) -> p g c j i", i=4),
+        )
+        for n in range(8):
+            if n + 2 < 8:
+                sigmoid_tile(1, n + 2)
+            gated_tile(1, n)
+            if n == 1:
+                nc.vector.quantize_mx(
+                    out=w2_codes[:].bitcast(FP8X4),
+                    scales=w2_scales[:],
+                    in_=grouped_w2[:].rearrange("p g n j -> p (g n j)"),
+                )
+            if n >= 2 and n % 2 == 0:
+                c = n // 2 - 1
+                quantise_hidden(1, c * CHUNK, (c + 1) * CHUNK)
+                second_layer(c)
+            if n >= 3 and n % 2 == 1 and n < 7:
+                scatter(n // 2 - 1)
+        quantise_hidden(1, 3 * CHUNK, 4 * CHUNK)
+        second_layer(3)
+        scatter(2)
+        scatter(3)
+        nc.sync.dma_start(out=out, in_=result[:])

@@ -50,12 +50,15 @@ def tile_picked_depth_glu_sigmoid_srt_p_kernel(
 
         raw = {}
 
-        def load_first_layer(name, w, g):
+        def load_first_layer(name, w, g, pieces=1):
             raw[name, g] = sb([P, PACK, PASS], F32, "raw_%s_%d" % (name, g))
-            nc.sync.dma_start(
-                out=raw[name, g][:],
-                in_=w.rearrange("(p j) c -> p j c", j=PACK)[:, :, g * PASS : (g + 1) * PASS],
-            )
+            rows = w.rearrange("(p j) c -> p j c", j=PACK)
+            width = PASS // pieces
+            for lo in range(0, PASS, width):
+                nc.sync.dma_start(
+                    out=raw[name, g][:, :, lo : lo + width],
+                    in_=rows[:, :, g * PASS + lo : g * PASS + lo + width],
+                )
 
         nc.sync.dma_start(offsets[:], offs)
         load_first_layer("w1", w1, 0)
@@ -66,11 +69,14 @@ def tile_picked_depth_glu_sigmoid_srt_p_kernel(
         nc.sync.dma_start(
             out=word_window[:].bitcast(I32), in_=x_words[0].rearrange("p n t -> p (n t)").bitcast(I32)
         )
-        load_first_layer("w3", w3, 0)
+        load_first_layer("w3", w3, 0, pieces=2)
         load_first_layer("w1", w1, 1)
         load_first_layer("w3", w3, 1)
         raw_w2 = sb([P, 2, PACK, N], F32, "raw_w2")
-        nc.sync.dma_start(out=raw_w2[:], in_=w2.rearrange("(g p j) n -> p g j n", g=2, j=PACK))
+        w2_rows = w2.rearrange("(g q t r) n -> g t q r n", g=2, t=PACK, r=8)
+        for g in range(2):
+            for t in range(PACK):
+                nc.sync.dma_start(out=raw_w2[:, g, t, :], in_=w2_rows[g, t])
         gates = sb([P, S], F32, "gates")
         nc.sync.dma_start(out=gates[:], in_=gate)
 
@@ -83,8 +89,8 @@ def tile_picked_depth_glu_sigmoid_srt_p_kernel(
 
         def cast(copy, name, g, m_lo, m_hi):
             copy(
-                out=grouped[name, g][:, :, m_lo:m_hi, :].rearrange("p t m j -> p m j t"),
-                in_=raw[name, g][:, :, PACK * m_lo : PACK * m_hi].rearrange("p j (m t) -> p m j t", t=PACK),
+                out=grouped[name, g][:, :, m_lo:m_hi, :].rearrange("p t (q r) j -> p q t r j", r=8),
+                in_=raw[name, g][:, :, PACK * m_lo : PACK * m_hi].rearrange("p j (q t r) -> p q t r j", t=PACK, r=8),
             )
 
         def quantise_weights(name, g, t_lo, t_hi):
@@ -149,9 +155,9 @@ def tile_picked_depth_glu_sigmoid_srt_p_kernel(
         w2_scales = sb([P, 2 * N], U8, "w2_scales")
         y = sb([P, S], F32, "y")
 
-        def second_layer(c):
-            toks = slice(c * CHUNK, (c + 1) * CHUNK)
-            bank = psum.tile([P, CHUNK], F32, name="bank_y", tag="bank_y", bufs=2)
+        def second_layer(lo, hi):
+            toks = slice(lo, hi)
+            bank = psum.tile([P, hi - lo], F32, name="bank_y", tag="bank_y", bufs=2)
             for g in range(2):
                 cols = slice(g * N, (g + 1) * N)
                 nc.tensor.matmul_mx(
@@ -169,41 +175,38 @@ def tile_picked_depth_glu_sigmoid_srt_p_kernel(
             lo, hi = c * CHUNK, (c + 1) * CHUNK
             nc.vector.tensor_tensor(result[:].indirect(entries(lo, hi)), y[:, lo:hi], gates[:, lo:hi], MULT)
 
-        nc.vector.tensor_copy(x_bytes[:], scale_window[:].bitcast(U8).indirect(offsets[:]))
         cast(nc.vector.tensor_copy, "w1", 0, 0, P)
+        nc.vector.tensor_copy(x_bytes[:], scale_window[:].bitcast(U8).indirect(offsets[:]))
         quantise_weights("w1", 0, 0, PACK)
         gather_words(0, 256)
         gather_words(256, 512)
         gather_words(512, 1024)
-        sigmoid_tile(0, 0)
-        sigmoid_tile(0, 1)
-        cast(nc.vector.tensor_copy, "w3", 0, 0, 84)
-        cast(nc.scalar.copy, "w3", 0, 84, P)
+        for n in range(8):
+            sigmoid_tile(0, n)
+        cast(nc.vector.tensor_copy, "w3", 0, 0, 64)
+        cast(nc.vector.tensor_copy, "w3", 0, 64, P)
         quantise_weights("w3", 0, 0, 2)
         quantise_weights("w3", 0, 2, 4)
-        for n in range(2, 8):
-            sigmoid_tile(0, n)
         cast(nc.scalar.copy, "w1", 1, 0, P)
+        cast(nc.scalar.copy, "w3", 1, 0, P)
         for n in range(5):
             gated_tile(0, n)
         quantise_hidden(0, 0, 512)
         for n in range(5, 8):
             gated_tile(0, n)
         quantise_weights("w1", 1, 0, PACK)
-        cast(nc.scalar.copy, "w3", 1, 32, P)
-        cast(nc.vector.tensor_copy, "w3", 1, 0, 32)
         quantise_hidden(0, 512, 1024)
         sigmoid_tile(1, 0)
         sigmoid_tile(1, 1)
-        quantise_weights("w3", 1, 0, 2)
-        quantise_weights("w3", 1, 2, 4)
-        nc.scalar.copy(
-            out=grouped_w2[:].rearrange("p g (c i) j -> p g c j i", i=4),
-            in_=raw_w2[:].rearrange("p g j (c i) -> p g c j i", i=4),
-        )
+        quantise_weights("w3", 1, 0, PACK)
         for n in range(8):
             if n + 2 < 8:
                 sigmoid_tile(1, n + 2)
+            if n == 0:
+                nc.scalar.copy(
+                    out=grouped_w2[:].rearrange("p g (c i) j -> p g c j i", i=4),
+                    in_=raw_w2[:].rearrange("p g j (c i) -> p g c j i", i=4),
+                )
             gated_tile(1, n)
             if n == 1:
                 nc.vector.quantize_mx(
@@ -212,13 +215,14 @@ def tile_picked_depth_glu_sigmoid_srt_p_kernel(
                     in_=grouped_w2[:].rearrange("p g n j -> p (g n j)"),
                 )
             if n >= 2 and n % 2 == 0:
-                c = n // 2 - 1
-                quantise_hidden(1, c * CHUNK, (c + 1) * CHUNK)
-                second_layer(c)
+                lo = (n - 2) * TOK
+                quantise_hidden(1, lo, lo + CHUNK)
+                second_layer(lo, lo + CHUNK)
             if n >= 3 and n % 2 == 1 and n < 7:
                 scatter(n // 2 - 1)
-        quantise_hidden(1, 3 * CHUNK, 4 * CHUNK)
-        second_layer(3)
+        for n in (6, 7):
+            quantise_hidden(1, n * TOK, (n + 1) * TOK)
+            second_layer(n * TOK, (n + 1) * TOK)
         scatter(2)
         scatter(3)
         nc.sync.dma_start(out=out, in_=result[:])

@@ -40,35 +40,35 @@ def tile_picked_depth_glu_sigmoid_srt_p_kernel(
             return offsets[:, lo // 16 : hi // 16]
 
         scale_window = sb([P, T // 4], I32, "scale_window")
-        nc.vector.memset(scale_window[:], 0)
         result = sb([P, T], F32, "result")
         nc.vector.memset(result[:], 0.0)
-        warm = sb([P, 2], F32, "warm")
-        nc.vector.memset(warm[:, 0:1], 0.0)
+        warm = sb([P, 1], F32, "warm")
+        nc.scalar.activation(out=warm[:], in_=result[:, 0:1], func=SIGMOID)
 
-        nc.scalar.activation(out=warm[:, 1:2], in_=warm[:, 0:1], func=SIGMOID)
 
         raw = {}
 
         def load_first_layer(name, w, g, pieces=1):
-            raw[name, g] = sb([P, PACK, PASS], F32, "raw_%s_%d" % (name, g))
             rows = w.rearrange("(p j) c -> p j c", j=PACK)
             width = PASS // pieces
-            for lo in range(0, PASS, width):
-                nc.sync.dma_start(
-                    out=raw[name, g][:, :, lo : lo + width],
-                    in_=rows[:, :, g * PASS + lo : g * PASS + lo + width],
-                )
+            raw[name, g] = []
+            for lo in range(g * PASS, (g + 1) * PASS, width):
+                piece = sb([P, PACK, width], F32, "raw_%s_%d" % (name, lo))
+                nc.sync.dma_start(out=piece[:], in_=rows[:, :, lo : lo + width])
+                raw[name, g].append(piece)
 
         nc.sync.dma_start(offsets[:], offs)
-        load_first_layer("w1", w1, 0)
         scale_rows = x_scales[0].bitcast(I32)
         for q in range(4):
-            nc.sync.dma_start(out=scale_window[32 * q : 32 * q + 4, :], in_=scale_rows[4 * q : 4 * q + 4, :])
+            nc.sync.dma_start(
+                out=scale_window[32 * q : 32 * q + 32, :],
+                in_=scale_rows[4 * q : 4 * q + 4, :].unsqueeze(0).to_broadcast([8, 4, T // 4]),
+            )
         word_window = sb([P, T], U32, "word_window")
         nc.sync.dma_start(
             out=word_window[:].bitcast(I32), in_=x_words[0].rearrange("p n t -> p (n t)").bitcast(I32)
         )
+        load_first_layer("w1", w1, 0)
         load_first_layer("w3", w3, 0, pieces=2)
         load_first_layer("w1", w1, 1)
         load_first_layer("w3", w3, 1)
@@ -87,11 +87,16 @@ def tile_picked_depth_glu_sigmoid_srt_p_kernel(
                 codes[name, g] = sb([P, PASS], U32, "codes_%s_%d" % (name, g))
                 scales[name, g] = sb([P, PASS], U8, "scales_%s_%d" % (name, g))
 
-        def cast(copy, name, g, m_lo, m_hi):
-            copy(
-                out=grouped[name, g][:, :, m_lo:m_hi, :].rearrange("p t (q r) j -> p q t r j", r=8),
-                in_=raw[name, g][:, :, PACK * m_lo : PACK * m_hi].rearrange("p j (q t r) -> p q t r j", t=PACK, r=8),
-            )
+        def cast(copy, name, g, t_lo, t_hi):
+            pieces = raw[name, g]
+            cols = P // len(pieces)
+            for i, piece in enumerate(pieces):
+                copy(
+                    out=grouped[name, g][:, t_lo:t_hi, i * cols : (i + 1) * cols, :].rearrange(
+                        "p t (q r) j -> p q t r j", r=8
+                    ),
+                    in_=piece[:].rearrange("p j (q t r) -> p q t r j", t=PACK, r=8)[:, :, t_lo:t_hi],
+                )
 
         def quantise_weights(name, g, t_lo, t_hi):
             cols = slice(t_lo * P, t_hi * P)
@@ -103,9 +108,6 @@ def tile_picked_depth_glu_sigmoid_srt_p_kernel(
 
         x_codes = sb([P, S], U32, "x_codes")
         x_bytes = sb([P, S], U8, "x_bytes")
-
-        def gather_words(lo, hi):
-            nc.vector.tensor_copy(x_codes[:, lo:hi], word_window[:].indirect(entries(lo, hi)))
 
         def first_layer(name, g, n, bufs):
             bank = psum.tile([P, PACK, TOK], F32, name="bank_" + name, tag="bank_" + name, bufs=bufs)
@@ -175,30 +177,32 @@ def tile_picked_depth_glu_sigmoid_srt_p_kernel(
             lo, hi = c * CHUNK, (c + 1) * CHUNK
             nc.vector.tensor_tensor(result[:].indirect(entries(lo, hi)), y[:, lo:hi], gates[:, lo:hi], MULT)
 
-        cast(nc.vector.tensor_copy, "w1", 0, 0, P)
         nc.vector.tensor_copy(x_bytes[:], scale_window[:].bitcast(U8).indirect(offsets[:]))
-        quantise_weights("w1", 0, 0, PACK)
-        gather_words(0, 256)
-        gather_words(256, 512)
-        gather_words(512, 1024)
+        nc.vector.tensor_copy(x_codes[:], word_window[:].indirect(offsets[:]))
+        cast(nc.scalar.copy, "w1", 0, 2, 4)
+        cast(nc.vector.tensor_copy, "w1", 0, 0, 2)
+        quantise_weights("w1", 0, 0, 2)
+        quantise_weights("w1", 0, 2, 4)
         for n in range(8):
             sigmoid_tile(0, n)
-        cast(nc.vector.tensor_copy, "w3", 0, 0, 64)
-        cast(nc.vector.tensor_copy, "w3", 0, 64, P)
+        cast(nc.vector.tensor_copy, "w3", 0, 0, PACK)
         quantise_weights("w3", 0, 0, 2)
         quantise_weights("w3", 0, 2, 4)
-        cast(nc.scalar.copy, "w1", 1, 0, P)
-        cast(nc.scalar.copy, "w3", 1, 0, P)
+        cast(nc.scalar.copy, "w1", 1, 0, PACK)
+        cast(nc.scalar.copy, "w3", 1, 1, PACK)
         for n in range(5):
             gated_tile(0, n)
         quantise_hidden(0, 0, 512)
-        for n in range(5, 8):
-            gated_tile(0, n)
+        gated_tile(0, 5)
         quantise_weights("w1", 1, 0, PACK)
-        quantise_hidden(0, 512, 1024)
+        gated_tile(0, 6)
+        cast(nc.vector.tensor_copy, "w3", 1, 0, 1)
+        gated_tile(0, 7)
         sigmoid_tile(1, 0)
         sigmoid_tile(1, 1)
-        quantise_weights("w3", 1, 0, PACK)
+        quantise_weights("w3", 1, 0, 2)
+        quantise_weights("w3", 1, 2, 4)
+        quantise_hidden(0, 512, 1024)
         for n in range(8):
             if n + 2 < 8:
                 sigmoid_tile(1, n + 2)
@@ -220,9 +224,13 @@ def tile_picked_depth_glu_sigmoid_srt_p_kernel(
                 second_layer(lo, lo + CHUNK)
             if n >= 3 and n % 2 == 1 and n < 7:
                 scatter(n // 2 - 1)
+            if n == 5:
+                settled = sb([P, 2 * CHUNK], F32, "settled")
+                nc.scalar.copy(out=settled[:], in_=result[:, : 2 * CHUNK])
+                nc.sync.dma_start(out=out[:, : 2 * CHUNK], in_=settled[:])
         for n in (6, 7):
             quantise_hidden(1, n * TOK, (n + 1) * TOK)
             second_layer(n * TOK, (n + 1) * TOK)
         scatter(2)
         scatter(3)
-        nc.sync.dma_start(out=out, in_=result[:])
+        nc.sync.dma_start(out=out[:, 2 * CHUNK :], in_=result[:, 2 * CHUNK :])

@@ -40,6 +40,7 @@ def tile_picked_depth_glu_sigmoid_srt_p_kernel(
             return offsets[:, lo // 16 : hi // 16]
 
         scale_window = sb([P, T // 4], I32, "scale_window")
+        nc.vector.memset(scale_window[:], 0)
         result = sb([P, T], F32, "result")
         nc.vector.memset(result[:], 0.0)
         warm = sb([P, 1], F32, "warm")
@@ -60,14 +61,11 @@ def tile_picked_depth_glu_sigmoid_srt_p_kernel(
         nc.sync.dma_start(offsets[:], offs)
         scale_rows = x_scales[0].bitcast(I32)
         for q in range(4):
-            nc.sync.dma_start(
-                out=scale_window[32 * q : 32 * q + 32, :],
-                in_=scale_rows[4 * q : 4 * q + 4, :].unsqueeze(0).to_broadcast([8, 4, T // 4]),
-            )
+            nc.sync.dma_start(out=scale_window[32 * q : 32 * q + 4, :], in_=scale_rows[4 * q : 4 * q + 4, :])
         word_window = sb([P, T], U32, "word_window")
-        nc.sync.dma_start(
-            out=word_window[:].bitcast(I32), in_=x_words[0].rearrange("p n t -> p (n t)").bitcast(I32)
-        )
+        word_rows = x_words[0].rearrange("p n t -> p (n t)").bitcast(I32)
+        for lo in range(0, T, T // 4):
+            nc.sync.dma_start(out=word_window[:, lo : lo + T // 4].bitcast(I32), in_=word_rows[:, lo : lo + T // 4])
         load_first_layer("w1", w1, 0)
         load_first_layer("w3", w3, 0, pieces=2)
         load_first_layer("w1", w1, 1)

@@ -40,7 +40,8 @@ def tile_picked_depth_glu_sigmoid_srt_p_kernel(
             return offsets[:, lo // 16 : hi // 16]
 
         scale_window = sb([P, T // 4], I32, "scale_window")
-        nc.vector.memset(scale_window[:], 0)
+        nc.vector.memset(scale_window[:, : T // 8], 0)
+        nc.gpsimd.memset(scale_window[:, T // 8 :], 0)
         result = sb([P, T], F32, "result")
         nc.vector.memset(result[:], 0.0)
         warm = sb([P, 1], F32, "warm")
@@ -64,8 +65,8 @@ def tile_picked_depth_glu_sigmoid_srt_p_kernel(
             nc.sync.dma_start(out=scale_window[32 * q : 32 * q + 4, :], in_=scale_rows[4 * q : 4 * q + 4, :])
         word_window = sb([P, T], U32, "word_window")
         word_rows = x_words[0].rearrange("p n t -> p (n t)").bitcast(I32)
-        for lo in range(0, T, T // 4):
-            nc.sync.dma_start(out=word_window[:, lo : lo + T // 4].bitcast(I32), in_=word_rows[:, lo : lo + T // 4])
+        for lo in range(0, T, T // 2):
+            nc.sync.dma_start(out=word_window[:, lo : lo + T // 2].bitcast(I32), in_=word_rows[:, lo : lo + T // 2])
         load_first_layer("w1", w1, 0)
         load_first_layer("w3", w3, 0, pieces=2)
         load_first_layer("w1", w1, 1)
@@ -85,16 +86,14 @@ def tile_picked_depth_glu_sigmoid_srt_p_kernel(
                 codes[name, g] = sb([P, PASS], U32, "codes_%s_%d" % (name, g))
                 scales[name, g] = sb([P, PASS], U8, "scales_%s_%d" % (name, g))
 
-        def cast(copy, name, g, t_lo, t_hi):
-            pieces = raw[name, g]
-            cols = P // len(pieces)
-            for i, piece in enumerate(pieces):
-                copy(
-                    out=grouped[name, g][:, t_lo:t_hi, i * cols : (i + 1) * cols, :].rearrange(
-                        "p t (q r) j -> p q t r j", r=8
-                    ),
-                    in_=piece[:].rearrange("p j (q t r) -> p q t r j", t=PACK, r=8)[:, :, t_lo:t_hi],
-                )
+        def cast(copy, name, g, t_lo, t_hi, i=0):
+            cols = P // len(raw[name, g])
+            copy(
+                out=grouped[name, g][:, t_lo:t_hi, i * cols : (i + 1) * cols, :].rearrange(
+                    "p t (q r) j -> p q t r j", r=8
+                ),
+                in_=raw[name, g][i][:].rearrange("p j (q t r) -> p q t r j", t=PACK, r=8)[:, :, t_lo:t_hi],
+            )
 
         def quantise_weights(name, g, t_lo, t_hi):
             cols = slice(t_lo * P, t_hi * P)
@@ -181,21 +180,23 @@ def tile_picked_depth_glu_sigmoid_srt_p_kernel(
         cast(nc.vector.tensor_copy, "w1", 0, 0, 2)
         quantise_weights("w1", 0, 0, 2)
         quantise_weights("w1", 0, 2, 4)
-        for n in range(8):
+        cast(nc.scalar.copy, "w3", 0, 0, PACK, 0)
+        cast(nc.vector.tensor_copy, "w3", 0, 0, PACK, 1)
+        for n in range(3):
             sigmoid_tile(0, n)
-        cast(nc.vector.tensor_copy, "w3", 0, 0, PACK)
         quantise_weights("w3", 0, 0, 2)
         quantise_weights("w3", 0, 2, 4)
-        cast(nc.scalar.copy, "w1", 1, 0, PACK)
-        cast(nc.scalar.copy, "w3", 1, 1, PACK)
         for n in range(5):
             gated_tile(0, n)
+            sigmoid_tile(0, n + 3)
+            if n == 1:
+                cast(nc.scalar.copy, "w1", 1, 0, PACK)
+        cast(nc.scalar.copy, "w3", 1, 2, 4)
         quantise_hidden(0, 0, 512)
-        gated_tile(0, 5)
+        cast(nc.vector.tensor_copy, "w3", 1, 0, 2)
         quantise_weights("w1", 1, 0, PACK)
-        gated_tile(0, 6)
-        cast(nc.vector.tensor_copy, "w3", 1, 0, 1)
-        gated_tile(0, 7)
+        for n in range(5, 8):
+            gated_tile(0, n)
         sigmoid_tile(1, 0)
         sigmoid_tile(1, 1)
         quantise_weights("w3", 1, 0, 2)

@@ -40,8 +40,7 @@ def tile_picked_depth_glu_sigmoid_srt_p_kernel(
             return offsets[:, lo // 16 : hi // 16]
 
         scale_window = sb([P, T // 4], I32, "scale_window")
-        nc.vector.memset(scale_window[:, : T // 8], 0)
-        nc.gpsimd.memset(scale_window[:, T // 8 :], 0)
+        nc.vector.memset(scale_window[:], 0)
         result = sb([P, T], F32, "result")
         nc.vector.memset(result[:], 0.0)
         warm = sb([P, 1], F32, "warm")
@@ -50,32 +49,31 @@ def tile_picked_depth_glu_sigmoid_srt_p_kernel(
 
         raw = {}
 
-        def load_first_layer(name, w, g, pieces=1):
+        def load_first_layer(name, w, g, pieces=1, i=0):
             rows = w.rearrange("(p j) c -> p j c", j=PACK)
             width = PASS // pieces
-            raw[name, g] = []
-            for lo in range(g * PASS, (g + 1) * PASS, width):
-                piece = sb([P, PACK, width], F32, "raw_%s_%d" % (name, lo))
-                nc.sync.dma_start(out=piece[:], in_=rows[:, :, lo : lo + width])
-                raw[name, g].append(piece)
+            lo = g * PASS + i * width
+            piece = sb([P, PACK, width], F32, "raw_%s_%d" % (name, lo))
+            nc.sync.dma_start(out=piece[:], in_=rows[:, :, lo : lo + width])
+            raw[name, g, i] = piece
 
+        load_first_layer("w1", w1, 0, 2, 0)
         nc.sync.dma_start(offsets[:], offs)
         scale_rows = x_scales[0].bitcast(I32)
         for q in range(4):
             nc.sync.dma_start(out=scale_window[32 * q : 32 * q + 4, :], in_=scale_rows[4 * q : 4 * q + 4, :])
+        load_first_layer("w1", w1, 0, 2, 1)
+        load_first_layer("w3", w3, 0, 2, 0)
+        load_first_layer("w3", w3, 0, 2, 1)
         word_window = sb([P, T], U32, "word_window")
         word_rows = x_words[0].rearrange("p n t -> p (n t)").bitcast(I32)
-        for lo in range(0, T, T // 2):
-            nc.sync.dma_start(out=word_window[:, lo : lo + T // 2].bitcast(I32), in_=word_rows[:, lo : lo + T // 2])
-        load_first_layer("w1", w1, 0)
-        load_first_layer("w3", w3, 0, pieces=2)
+        reach = T - S + CHUNK
+        for lo, hi in ((0, reach), (reach, T)):
+            nc.sync.dma_start(out=word_window[:, lo:hi].bitcast(I32), in_=word_rows[:, lo:hi])
         load_first_layer("w1", w1, 1)
         load_first_layer("w3", w3, 1)
         raw_w2 = sb([P, 2, PACK, N], F32, "raw_w2")
-        w2_rows = w2.rearrange("(g q t r) n -> g t q r n", g=2, t=PACK, r=8)
-        for g in range(2):
-            for t in range(PACK):
-                nc.sync.dma_start(out=raw_w2[:, g, t, :], in_=w2_rows[g, t])
+        nc.sync.dma_start(out=raw_w2[:], in_=w2.rearrange("(g p j) n -> p g j n", g=2, j=PACK))
         gates = sb([P, S], F32, "gates")
         nc.sync.dma_start(out=gates[:], in_=gate)
 
@@ -87,12 +85,12 @@ def tile_picked_depth_glu_sigmoid_srt_p_kernel(
                 scales[name, g] = sb([P, PASS], U8, "scales_%s_%d" % (name, g))
 
         def cast(copy, name, g, t_lo, t_hi, i=0):
-            cols = P // len(raw[name, g])
+            cols = raw[name, g, i].shape[2] // PACK
             copy(
                 out=grouped[name, g][:, t_lo:t_hi, i * cols : (i + 1) * cols, :].rearrange(
-                    "p t (q r) j -> p q t r j", r=8
+                    "p t (a r) j -> p a j r t", r=2
                 ),
-                in_=raw[name, g][i][:].rearrange("p j (q t r) -> p q t r j", t=PACK, r=8)[:, :, t_lo:t_hi],
+                in_=raw[name, g, i][:].rearrange("p j (a r t) -> p a j r t", t=PACK, r=2)[:, :, :, :, t_lo:t_hi],
             )
 
         def quantise_weights(name, g, t_lo, t_hi):
@@ -175,32 +173,34 @@ def tile_picked_depth_glu_sigmoid_srt_p_kernel(
             nc.vector.tensor_tensor(result[:].indirect(entries(lo, hi)), y[:, lo:hi], gates[:, lo:hi], MULT)
 
         nc.vector.tensor_copy(x_bytes[:], scale_window[:].bitcast(U8).indirect(offsets[:]))
-        nc.vector.tensor_copy(x_codes[:], word_window[:].indirect(offsets[:]))
-        cast(nc.scalar.copy, "w1", 0, 2, 4)
-        cast(nc.vector.tensor_copy, "w1", 0, 0, 2)
-        quantise_weights("w1", 0, 0, 2)
-        quantise_weights("w1", 0, 2, 4)
+        cast(nc.scalar.copy, "w1", 0, 0, PACK, 0)
+        cast(nc.scalar.copy, "w1", 0, 0, PACK, 1)
+        quantise_weights("w1", 0, 0, PACK)
         cast(nc.scalar.copy, "w3", 0, 0, PACK, 0)
         cast(nc.vector.tensor_copy, "w3", 0, 0, PACK, 1)
-        for n in range(3):
+        quantise_weights("w3", 0, 0, PACK)
+        nc.vector.tensor_copy(x_codes[:, :CHUNK], word_window[:, :reach].indirect(entries(0, CHUNK)))
+        for lo in range(CHUNK, S, CHUNK):
+            nc.vector.tensor_copy(x_codes[:, lo : lo + CHUNK], word_window[:].indirect(entries(lo, lo + CHUNK)))
+        for n in range(2):
             sigmoid_tile(0, n)
-        quantise_weights("w3", 0, 0, 2)
-        quantise_weights("w3", 0, 2, 4)
-        for n in range(5):
+        for n in range(4):
             gated_tile(0, n)
-            sigmoid_tile(0, n + 3)
-            if n == 1:
-                cast(nc.scalar.copy, "w1", 1, 0, PACK)
-        cast(nc.scalar.copy, "w3", 1, 2, 4)
+            sigmoid_tile(0, n + 2)
+        cast(nc.vector.tensor_copy, "w1", 1, 0, PACK)
         quantise_hidden(0, 0, 512)
-        cast(nc.vector.tensor_copy, "w3", 1, 0, 2)
         quantise_weights("w1", 1, 0, PACK)
-        for n in range(5, 8):
+        for n in range(4, 6):
+            gated_tile(0, n)
+            sigmoid_tile(0, n + 2)
+        cast(nc.scalar.copy, "w3", 1, 0, 2)
+        cast(nc.scalar.copy, "w3", 1, 2, 4)
+        quantise_weights("w3", 1, 0, 2)
+        quantise_weights("w3", 1, 2, 4)
+        for n in range(6, 8):
             gated_tile(0, n)
         sigmoid_tile(1, 0)
         sigmoid_tile(1, 1)
-        quantise_weights("w3", 1, 0, 2)
-        quantise_weights("w3", 1, 2, 4)
         quantise_hidden(0, 512, 1024)
         for n in range(8):
             if n + 2 < 8:
@@ -221,9 +221,9 @@ def tile_picked_depth_glu_sigmoid_srt_p_kernel(
                 lo = (n - 2) * TOK
                 quantise_hidden(1, lo, lo + CHUNK)
                 second_layer(lo, lo + CHUNK)
-            if n >= 3 and n % 2 == 1 and n < 7:
-                scatter(n // 2 - 1)
-            if n == 5:
+            if n >= 4 and n % 2 == 0:
+                scatter(n // 2 - 2)
+            if n == 6:
                 settled = sb([P, 2 * CHUNK], F32, "settled")
                 nc.scalar.copy(out=settled[:], in_=result[:, : 2 * CHUNK])
                 nc.sync.dma_start(out=out[:, : 2 * CHUNK], in_=settled[:])

@@ -13,6 +13,7 @@ U16 = mybir.dt.uint16
 U8 = mybir.dt.uint8
 FP8X4 = mybir.dt.float8_e4m3fn_x4
 MULT = mybir.AluOpType.mult
+ADD = mybir.AluOpType.add
 SIGMOID = mybir.ActivationFunctionType.Sigmoid
 
 P = 128
@@ -31,8 +32,8 @@ def tile_picked_depth_glu_sigmoid_srt_p_kernel(
         keep = ctx.enter_context(tc.tile_pool(name="keep", bufs=1))
         psum = ctx.enter_context(tc.psum_pool(name="psum", bufs=1))
 
-        def sb(shape, dtype, name):
-            return keep.tile(shape, dtype, name=name, align_bytes=64)
+        def sb(shape, dtype, name, tag=None):
+            return keep.tile(shape, dtype, name=name, tag=tag or name, align_bytes=64)
 
         offsets = lists.tile([P, S // 16], U16, name="offsets")
 
@@ -67,8 +68,8 @@ def tile_picked_depth_glu_sigmoid_srt_p_kernel(
         load_first_layer("w3", w3, 0, 2, 1)
         word_window = sb([P, T], U32, "word_window")
         word_rows = x_words[0].rearrange("p n t -> p (n t)").bitcast(I32)
-        reach = T - S + CHUNK
-        for lo, hi in ((0, reach), (reach, T)):
+        reach = [T - S + CHUNK, T - S + 2 * CHUNK, T, T]
+        for lo, hi in ((0, reach[0]), (reach[0], reach[1]), (reach[1], T)):
             nc.sync.dma_start(out=word_window[:, lo:hi].bitcast(I32), in_=word_rows[:, lo:hi])
         load_first_layer("w1", w1, 1)
         load_first_layer("w3", w3, 1)
@@ -91,6 +92,16 @@ def tile_picked_depth_glu_sigmoid_srt_p_kernel(
                     "p t (a r) j -> p a j r t", r=2
                 ),
                 in_=raw[name, g, i][:].rearrange("p j (a r t) -> p a j r t", t=PACK, r=2)[:, :, :, :, t_lo:t_hi],
+            )
+
+        def cast_on_gpsimd(name, g, lo, hi):
+            nc.gpsimd.tensor_scalar(
+                out=grouped[name, g][:, :, lo:hi, :].rearrange("p t m j -> p m t j"),
+                in0=raw[name, g, 0][:].rearrange("p j (m t) -> p m t j", t=PACK)[:, lo:hi],
+                scalar1=1.0,
+                scalar2=0.0,
+                op0=MULT,
+                op1=ADD,
             )
 
         def quantise_weights(name, g, t_lo, t_hi):
@@ -120,6 +131,19 @@ def tile_picked_depth_glu_sigmoid_srt_p_kernel(
                 )
             return bank
 
+        def keep_clock(tag, bufs, passes):
+            bank = psum.tile([P, PASS], F32, name=tag, tag=tag, bufs=bufs)
+            for i in range(passes):
+                nc.tensor.matmul_mx(
+                    out=bank[:],
+                    lhsT=codes["w1", 0][:, :P].bitcast(FP8X4),
+                    lhsT_scale=scales["w1", 0][:, :P],
+                    rhs=codes["w1", 0][:].bitcast(FP8X4),
+                    rhs_scale=scales["w1", 0][:],
+                    start=True,
+                    stop=True,
+                )
+
         sig = {}
 
         def sigmoid_tile(g, n):
@@ -128,7 +152,7 @@ def tile_picked_depth_glu_sigmoid_srt_p_kernel(
             nc.scalar.activation(out=sig[g, n][:], in_=bank[:].rearrange("p t n -> p n t"), func=SIGMOID)
 
         hidden = [sb([P, S, PACK], BF16, "hidden_%d" % g) for g in range(2)]
-        h_codes = [sb([P, S], U32, "h_codes_%d" % g) for g in range(2)]
+        h_codes = {}
         h_scales = [sb([P, S], U8, "h_scales_%d" % g) for g in range(2)]
 
         def gated_tile(g, n):
@@ -140,9 +164,16 @@ def tile_picked_depth_glu_sigmoid_srt_p_kernel(
                 op=MULT,
             )
 
-        def quantise_hidden(g, lo, hi):
+        def hidden_codes(g, lo, hi):
+            width = PASS if g == 0 else CHUNK
+            return h_codes[g, lo // width][:, lo % width : lo % width + hi - lo].bitcast(FP8X4)
+
+        def quantise_hidden(g, lo, hi, tag=None):
+            width = PASS if g == 0 else CHUNK
+            if lo % width == 0:
+                h_codes[g, lo // width] = sb([P, width], U32, "h_codes_%d_%d" % (g, lo), tag)
             nc.vector.quantize_mx(
-                out=h_codes[g][:, lo:hi].bitcast(FP8X4),
+                out=hidden_codes(g, lo, hi),
                 scales=h_scales[g][:, lo:hi],
                 in_=hidden[g][:, lo:hi, :].rearrange("p n t -> p (n t)"),
             )
@@ -161,7 +192,7 @@ def tile_picked_depth_glu_sigmoid_srt_p_kernel(
                     out=bank[:],
                     lhsT=w2_codes[:, cols].bitcast(FP8X4),
                     lhsT_scale=w2_scales[:, cols],
-                    rhs=h_codes[g][:, toks].bitcast(FP8X4),
+                    rhs=hidden_codes(g, lo, hi),
                     rhs_scale=h_scales[g][:, toks],
                     start=(g == 0),
                     stop=(g == 1),
@@ -176,32 +207,38 @@ def tile_picked_depth_glu_sigmoid_srt_p_kernel(
         cast(nc.scalar.copy, "w1", 0, 0, PACK, 0)
         cast(nc.scalar.copy, "w1", 0, 0, PACK, 1)
         quantise_weights("w1", 0, 0, PACK)
-        cast(nc.scalar.copy, "w3", 0, 0, PACK, 0)
-        cast(nc.vector.tensor_copy, "w3", 0, 0, PACK, 1)
-        quantise_weights("w3", 0, 0, PACK)
-        nc.vector.tensor_copy(x_codes[:, :CHUNK], word_window[:, :reach].indirect(entries(0, CHUNK)))
-        for lo in range(CHUNK, S, CHUNK):
-            nc.vector.tensor_copy(x_codes[:, lo : lo + CHUNK], word_window[:].indirect(entries(lo, lo + CHUNK)))
+        keep_clock("bank_y", 2, 4)
+        for i in range(2):
+            cast(nc.scalar.copy, "w3", 0, 2, PACK, i)
+            cast(nc.vector.tensor_copy, "w3", 0, 0, 2, i)
+        quantise_weights("w3", 0, 0, 2)
+        quantise_weights("w3", 0, 2, PACK)
+        for c in range(S // CHUNK):
+            lo, hi = c * CHUNK, (c + 1) * CHUNK
+            nc.vector.tensor_copy(x_codes[:, lo:hi], word_window[:, : reach[c]].indirect(entries(lo, hi)))
         for n in range(2):
             sigmoid_tile(0, n)
         for n in range(4):
             gated_tile(0, n)
             sigmoid_tile(0, n + 2)
-        cast(nc.vector.tensor_copy, "w1", 1, 0, PACK)
+        cast(nc.vector.tensor_copy, "w1", 1, 0, 3)
+        cast(nc.scalar.copy, "w1", 1, 3, PACK)
         quantise_hidden(0, 0, 512)
-        quantise_weights("w1", 1, 0, PACK)
         for n in range(4, 6):
             gated_tile(0, n)
             sigmoid_tile(0, n + 2)
+        quantise_weights("w1", 1, 0, PACK)
         cast(nc.scalar.copy, "w3", 1, 0, 2)
         cast(nc.scalar.copy, "w3", 1, 2, 4)
         quantise_weights("w3", 1, 0, 2)
         quantise_weights("w3", 1, 2, 4)
         for n in range(6, 8):
             gated_tile(0, n)
+        for i in range(3):
+            keep_clock("bank_w3", 3, 1)
         sigmoid_tile(1, 0)
         sigmoid_tile(1, 1)
-        quantise_hidden(0, 512, 1024)
+        quantise_hidden(0, 512, 1024, "raw_w3_512")
         for n in range(8):
             if n + 2 < 8:
                 sigmoid_tile(1, n + 2)
@@ -224,7 +261,7 @@ def tile_picked_depth_glu_sigmoid_srt_p_kernel(
             if n >= 4 and n % 2 == 0:
                 scatter(n // 2 - 2)
             if n == 6:
-                settled = sb([P, 2 * CHUNK], F32, "settled")
+                settled = sb([P, 2 * CHUNK], F32, "settled", "h_codes_1_512")
                 nc.scalar.copy(out=settled[:], in_=result[:, : 2 * CHUNK])
                 nc.sync.dma_start(out=out[:, : 2 * CHUNK], in_=settled[:])
         for n in (6, 7):

@@ -218,22 +218,18 @@ def tile_picked_depth_glu_sigmoid_srt_p_kernel(
             nc.vector.tensor_copy(x_codes[:, lo:hi], word_window[:, : reach[c]].indirect(entries(lo, hi)))
         for n in range(2):
             sigmoid_tile(0, n)
-        for n in range(4):
+        for lo in range(0, P, P // 2):
+            cast_on_gpsimd("w1", 1, lo, lo + P // 2)
+        for n in range(8):
             gated_tile(0, n)
-            sigmoid_tile(0, n + 2)
-        cast(nc.vector.tensor_copy, "w1", 1, 0, 3)
-        cast(nc.scalar.copy, "w1", 1, 3, PACK)
-        quantise_hidden(0, 0, 512)
-        for n in range(4, 6):
-            gated_tile(0, n)
-            sigmoid_tile(0, n + 2)
+            if n + 2 < 8:
+                sigmoid_tile(0, n + 2)
         quantise_weights("w1", 1, 0, PACK)
         cast(nc.scalar.copy, "w3", 1, 0, 2)
         cast(nc.scalar.copy, "w3", 1, 2, 4)
+        quantise_hidden(0, 0, 512, "raw_w1_512")
         quantise_weights("w3", 1, 0, 2)
         quantise_weights("w3", 1, 2, 4)
-        for n in range(6, 8):
-            gated_tile(0, n)
         for i in range(3):
             keep_clock("bank_w3", 3, 1)
         sigmoid_tile(1, 0)

@@ -50,54 +50,66 @@ def tile_picked_depth_glu_sigmoid_srt_p_kernel(
 
         raw = {}
 
-        def load_first_layer(name, w, g, pieces=1, i=0):
+        def load_first_layer(name, w, lo, hi):
             rows = w.rearrange("(p j) c -> p j c", j=PACK)
-            width = PASS // pieces
-            lo = g * PASS + i * width
-            piece = sb([P, PACK, width], F32, "raw_%s_%d" % (name, lo))
-            nc.sync.dma_start(out=piece[:], in_=rows[:, :, lo : lo + width])
-            raw[name, g, i] = piece
+            raw[name, lo] = sb([P, PACK, hi - lo], F32, "raw_%s_%d" % (name, lo))
+            nc.sync.dma_start(out=raw[name, lo][:], in_=rows[:, :, lo:hi])
 
-        load_first_layer("w1", w1, 0, 2, 0)
+        load_first_layer("w1", w1, 0, 256)
         nc.sync.dma_start(offsets[:], offs)
         scale_rows = x_scales[0].bitcast(I32)
         for q in range(4):
             nc.sync.dma_start(out=scale_window[32 * q : 32 * q + 4, :], in_=scale_rows[4 * q : 4 * q + 4, :])
-        load_first_layer("w1", w1, 0, 2, 1)
-        load_first_layer("w3", w3, 0, 2, 0)
-        load_first_layer("w3", w3, 0, 2, 1)
+        load_first_layer("w1", w1, 256, PASS)
+        load_first_layer("w3", w3, 0, 256)
+        load_first_layer("w3", w3, 256, PASS)
         word_window = sb([P, T], U32, "word_window")
         word_rows = x_words[0].rearrange("p n t -> p (n t)").bitcast(I32)
         reach = [T - S + CHUNK, T - S + 2 * CHUNK, T, T]
         for lo, hi in ((0, reach[0]), (reach[0], reach[1]), (reach[1], T)):
             nc.sync.dma_start(out=word_window[:, lo:hi].bitcast(I32), in_=word_rows[:, lo:hi])
-        load_first_layer("w1", w1, 1)
-        load_first_layer("w3", w3, 1)
+        load_first_layer("w1", w1, PASS, PASS + PASS // 2)
+        load_first_layer("w1", w1, PASS + PASS // 2, H)
+        load_first_layer("w3", w3, PASS, H)
         raw_w2 = sb([P, 2, PACK, N], F32, "raw_w2")
-        nc.sync.dma_start(out=raw_w2[:], in_=w2.rearrange("(g p j) n -> p g j n", g=2, j=PACK))
+        nc.sync.dma_start(out=raw_w2[:, 0], in_=w2[:PASS].rearrange("(p j) n -> p j n", j=PACK))
+        w2_rows = w2[PASS:].rearrange("(a t r) n -> t a r n", t=PACK, r=PACK)
+        for t in range(PACK):
+            nc.sync.dma_start(out=raw_w2[:, 1, t, :], in_=w2_rows[t])
         gates = sb([P, S], F32, "gates")
         nc.sync.dma_start(out=gates[:], in_=gate)
 
         grouped, codes, scales = {}, {}, {}
         for name in ("w1", "w3"):
             for g in range(2):
-                grouped[name, g] = sb([P, PACK, P, PACK], BF16, "grouped_%s_%d" % (name, g))
+                if (name, g) != ("w1", 1):
+                    grouped[name, g] = sb([P, PACK, P, PACK], BF16, "grouped_%s_%d" % (name, g))
                 codes[name, g] = sb([P, PASS], U32, "codes_%s_%d" % (name, g))
                 scales[name, g] = sb([P, PASS], U8, "scales_%s_%d" % (name, g))
 
-        def cast(copy, name, g, t_lo, t_hi, i=0):
-            cols = raw[name, g, i].shape[2] // PACK
+        def cast(copy, name, lo, t_lo, t_hi):
+            piece = raw[name, lo]
+            m_lo = lo % PASS // PACK
+            words = grouped[name, lo // PASS][:, t_lo:t_hi, m_lo : m_lo + piece.shape[2] // PACK, :]
+            if lo < PASS:
+                copy(
+                    out=words.rearrange("p t (a r) j -> p a j r t", r=2),
+                    in_=piece[:].rearrange("p j (a r t) -> p a j r t", t=PACK, r=2)[:, :, :, :, t_lo:t_hi],
+                )
+                return
             copy(
-                out=grouped[name, g][:, t_lo:t_hi, i * cols : (i + 1) * cols, :].rearrange(
-                    "p t (a r) j -> p a j r t", r=2
-                ),
-                in_=raw[name, g, i][:].rearrange("p j (a r t) -> p a j r t", t=PACK, r=2)[:, :, :, :, t_lo:t_hi],
+                out=words.rearrange("p t (a r) j -> p a t j r", r=PACK),
+                in_=piece[:].rearrange("p j (a t r) -> p a t j r", t=PACK, r=PACK)[:, :, t_lo:t_hi],
             )
 
-        def cast_on_gpsimd(name, g, lo, hi):
+        def cast_on_gpsimd(name, lo):
+            piece = raw[name, lo]
+            m_lo = lo % PASS // PACK
             nc.gpsimd.tensor_scalar(
-                out=grouped[name, g][:, :, lo:hi, :].rearrange("p t m j -> p m t j"),
-                in0=raw[name, g, 0][:].rearrange("p j (m t) -> p m t j", t=PACK)[:, lo:hi],
+                out=grouped[name, lo // PASS][:, :, m_lo : m_lo + piece.shape[2] // PACK, :].rearrange(
+                    "p t (a r) j -> p a t r j", r=PACK
+                ),
+                in0=piece[:].rearrange("p j (a t r) -> p a t r j", t=PACK, r=PACK),
                 scalar1=1.0,
                 scalar2=0.0,
                 op0=MULT,
@@ -204,13 +216,14 @@ def tile_picked_depth_glu_sigmoid_srt_p_kernel(
             nc.vector.tensor_tensor(result[:].indirect(entries(lo, hi)), y[:, lo:hi], gates[:, lo:hi], MULT)
 
         nc.vector.tensor_copy(x_bytes[:], scale_window[:].bitcast(U8).indirect(offsets[:]))
-        cast(nc.scalar.copy, "w1", 0, 0, PACK, 0)
-        cast(nc.scalar.copy, "w1", 0, 0, PACK, 1)
+        cast(nc.scalar.copy, "w1", 0, 0, PACK)
+        cast(nc.scalar.copy, "w1", 256, 0, PACK)
+        cast(nc.vector.tensor_copy, "w3", 0, 0, 2)
         quantise_weights("w1", 0, 0, PACK)
         keep_clock("bank_y", 2, 4)
-        for i in range(2):
-            cast(nc.scalar.copy, "w3", 0, 2, PACK, i)
-            cast(nc.vector.tensor_copy, "w3", 0, 0, 2, i)
+        cast(nc.scalar.copy, "w3", 0, 2, PACK)
+        cast(nc.scalar.copy, "w3", 256, 2, PACK)
+        cast(nc.vector.tensor_copy, "w3", 256, 0, 2)
         quantise_weights("w3", 0, 0, 2)
         quantise_weights("w3", 0, 2, PACK)
         for c in range(S // CHUNK):
@@ -218,16 +231,17 @@ def tile_picked_depth_glu_sigmoid_srt_p_kernel(
             nc.vector.tensor_copy(x_codes[:, lo:hi], word_window[:, : reach[c]].indirect(entries(lo, hi)))
         for n in range(2):
             sigmoid_tile(0, n)
-        for lo in range(0, P, P // 2):
-            cast_on_gpsimd("w1", 1, lo, lo + P // 2)
+        grouped["w1", 1] = sb([P, PACK, P, PACK], BF16, "grouped_w1_1", "word_window")
+        for lo in (PASS, PASS + PASS // 2):
+            cast_on_gpsimd("w1", lo)
         for n in range(8):
             gated_tile(0, n)
             if n + 2 < 8:
                 sigmoid_tile(0, n + 2)
         quantise_weights("w1", 1, 0, PACK)
-        cast(nc.scalar.copy, "w3", 1, 0, 2)
-        cast(nc.scalar.copy, "w3", 1, 2, 4)
-        quantise_hidden(0, 0, 512, "raw_w1_512")
+        cast(nc.scalar.copy, "w3", PASS, 0, 2)
+        cast(nc.scalar.copy, "w3", PASS, 2, 4)
+        quantise_hidden(0, 0, 512, "raw_w1_768")
         quantise_weights("w3", 1, 0, 2)
         quantise_weights("w3", 1, 2, 4)
         for i in range(3):

@@ -61,8 +61,8 @@ def tile_picked_depth_glu_sigmoid_srt_p_kernel(
         for q in range(4):
             nc.sync.dma_start(out=scale_window[32 * q : 32 * q + 4, :], in_=scale_rows[4 * q : 4 * q + 4, :])
         load_first_layer("w1", w1, 256, PASS)
-        load_first_layer("w3", w3, 0, 256)
-        load_first_layer("w3", w3, 256, PASS)
+        load_first_layer("w3", w3, 0, 192)
+        load_first_layer("w3", w3, 192, PASS)
         word_window = sb([P, T], U32, "word_window")
         word_rows = x_words[0].rearrange("p n t -> p (n t)").bitcast(I32)
         reach = [T - S + CHUNK, T - S + 2 * CHUNK, T, T]
@@ -72,10 +72,10 @@ def tile_picked_depth_glu_sigmoid_srt_p_kernel(
         load_first_layer("w1", w1, PASS + PASS // 2, H)
         load_first_layer("w3", w3, PASS, H)
         raw_w2 = sb([P, 2, PACK, N], F32, "raw_w2")
-        nc.sync.dma_start(out=raw_w2[:, 0], in_=w2[:PASS].rearrange("(p j) n -> p j n", j=PACK))
-        w2_rows = w2[PASS:].rearrange("(a t r) n -> t a r n", t=PACK, r=PACK)
+        w2_rows = w2[:PASS].rearrange("(a t r) n -> t a r n", t=PACK, r=PACK)
         for t in range(PACK):
-            nc.sync.dma_start(out=raw_w2[:, 1, t, :], in_=w2_rows[t])
+            nc.sync.dma_start(out=raw_w2[:, 0, t, :], in_=w2_rows[t])
+        nc.sync.dma_start(out=raw_w2[:, 1], in_=w2[PASS:].rearrange("(p j) n -> p j n", j=PACK))
         gates = sb([P, S], F32, "gates")
         nc.sync.dma_start(out=gates[:], in_=gate)
 
@@ -91,7 +91,7 @@ def tile_picked_depth_glu_sigmoid_srt_p_kernel(
             piece = raw[name, lo]
             m_lo = lo % PASS // PACK
             words = grouped[name, lo // PASS][:, t_lo:t_hi, m_lo : m_lo + piece.shape[2] // PACK, :]
-            if lo < PASS:
+            if lo >= PASS:
                 copy(
                     out=words.rearrange("p t (a r) j -> p a j r t", r=2),
                     in_=piece[:].rearrange("p j (a r t) -> p a j r t", t=PACK, r=2)[:, :, :, :, t_lo:t_hi],
@@ -106,10 +106,8 @@ def tile_picked_depth_glu_sigmoid_srt_p_kernel(
             piece = raw[name, lo]
             m_lo = lo % PASS // PACK
             nc.gpsimd.tensor_scalar(
-                out=grouped[name, lo // PASS][:, :, m_lo : m_lo + piece.shape[2] // PACK, :].rearrange(
-                    "p t (a r) j -> p a t r j", r=PACK
-                ),
-                in0=piece[:].rearrange("p j (a t r) -> p a t r j", t=PACK, r=PACK),
+                out=grouped[name, lo // PASS][:, :, m_lo : m_lo + piece.shape[2] // PACK, :].rearrange("p t m j -> p m t j"),
+                in0=piece[:].rearrange("p j (m t) -> p m t j", t=PACK),
                 scalar1=1.0,
                 scalar2=0.0,
                 op0=MULT,
@@ -222,8 +220,8 @@ def tile_picked_depth_glu_sigmoid_srt_p_kernel(
         quantise_weights("w1", 0, 0, PACK)
         keep_clock("bank_y", 2, 4)
         cast(nc.scalar.copy, "w3", 0, 2, PACK)
-        cast(nc.scalar.copy, "w3", 256, 2, PACK)
-        cast(nc.vector.tensor_copy, "w3", 256, 0, 2)
+        cast(nc.scalar.copy, "w3", 192, 2, PACK)
+        cast(nc.vector.tensor_copy, "w3", 192, 0, 2)
         quantise_weights("w3", 0, 0, 2)
         quantise_weights("w3", 0, 2, PACK)
         for c in range(S // CHUNK):

@@ -65,7 +65,8 @@ def tile_picked_depth_glu_sigmoid_srt_p_kernel(
         load_first_layer("w3", w3, 192, PASS)
         word_window = sb([P, T], U32, "word_window")
         word_rows = x_words[0].rearrange("p n t -> p (n t)").bitcast(I32)
-        reach = [T - S + CHUNK, T - S + 2 * CHUNK, T, T]
+        cuts = [0, 160, 416, 672, S]
+        reach = [T - S + hi for hi in cuts[1:]]
         for lo, hi in ((0, reach[0]), (reach[0], reach[1]), (reach[1], T)):
             nc.sync.dma_start(out=word_window[:, lo:hi].bitcast(I32), in_=word_rows[:, lo:hi])
         load_first_layer("w1", w1, PASS, PASS + PASS // 2)
@@ -87,27 +88,26 @@ def tile_picked_depth_glu_sigmoid_srt_p_kernel(
                 codes[name, g] = sb([P, PASS], U32, "codes_%s_%d" % (name, g))
                 scales[name, g] = sb([P, PASS], U8, "scales_%s_%d" % (name, g))
 
-        def cast(copy, name, lo, t_lo, t_hi):
-            piece = raw[name, lo]
-            m_lo = lo % PASS // PACK
+        def cast(copy, name, lo, t_lo, t_hi, skip=0):
+            piece = raw[name, lo][:, :, skip:]
+            m_lo = (lo + skip) % PASS // PACK
             words = grouped[name, lo // PASS][:, t_lo:t_hi, m_lo : m_lo + piece.shape[2] // PACK, :]
             if lo >= PASS:
                 copy(
                     out=words.rearrange("p t (a r) j -> p a j r t", r=2),
-                    in_=piece[:].rearrange("p j (a r t) -> p a j r t", t=PACK, r=2)[:, :, :, :, t_lo:t_hi],
+                    in_=piece.rearrange("p j (a r t) -> p a j r t", t=PACK, r=2)[:, :, :, :, t_lo:t_hi],
                 )
                 return
             copy(
                 out=words.rearrange("p t (a r) j -> p a t j r", r=PACK),
-                in_=piece[:].rearrange("p j (a t r) -> p a t j r", t=PACK, r=PACK)[:, :, t_lo:t_hi],
+                in_=piece.rearrange("p j (a t r) -> p a t j r", t=PACK, r=PACK)[:, :, t_lo:t_hi],
             )
 
-        def cast_on_gpsimd(name, lo):
-            piece = raw[name, lo]
+        def cast_on_gpsimd(name, lo, t_lo, m_hi):
             m_lo = lo % PASS // PACK
             nc.gpsimd.tensor_scalar(
-                out=grouped[name, lo // PASS][:, :, m_lo : m_lo + piece.shape[2] // PACK, :].rearrange("p t m j -> p m t j"),
-                in0=piece[:].rearrange("p j (m t) -> p m t j", t=PACK),
+                out=grouped[name, 1][:, t_lo:, m_lo:m_hi, :].rearrange("p t m j -> p m t j"),
+                in0=raw[name, lo][:].rearrange("p j (m t) -> p m t j", t=PACK)[:, : m_hi - m_lo, t_lo:],
                 scalar1=1.0,
                 scalar2=0.0,
                 op0=MULT,
@@ -218,27 +218,28 @@ def tile_picked_depth_glu_sigmoid_srt_p_kernel(
         cast(nc.scalar.copy, "w1", 256, 0, PACK)
         cast(nc.vector.tensor_copy, "w3", 0, 0, 2)
         quantise_weights("w1", 0, 0, PACK)
-        keep_clock("bank_y", 2, 4)
+        keep_clock("bank_y", 2, 3)
         cast(nc.scalar.copy, "w3", 0, 2, PACK)
         cast(nc.scalar.copy, "w3", 192, 2, PACK)
         cast(nc.vector.tensor_copy, "w3", 192, 0, 2)
         quantise_weights("w3", 0, 0, 2)
         quantise_weights("w3", 0, 2, PACK)
-        for c in range(S // CHUNK):
-            lo, hi = c * CHUNK, (c + 1) * CHUNK
+        for c in range(4):
+            lo, hi = cuts[c], cuts[c + 1]
             nc.vector.tensor_copy(x_codes[:, lo:hi], word_window[:, : reach[c]].indirect(entries(lo, hi)))
         for n in range(2):
             sigmoid_tile(0, n)
         grouped["w1", 1] = sb([P, PACK, P, PACK], BF16, "grouped_w1_1", "word_window")
-        for lo in (PASS, PASS + PASS // 2):
-            cast_on_gpsimd("w1", lo)
+        cast_on_gpsimd("w1", PASS, 0, P // 2)
+        cast_on_gpsimd("w1", PASS + PASS // 2, 0, P)
+        cast_on_gpsimd("w3", PASS, 2, 48)
         for n in range(8):
             gated_tile(0, n)
             if n + 2 < 8:
                 sigmoid_tile(0, n + 2)
         quantise_weights("w1", 1, 0, PACK)
         cast(nc.scalar.copy, "w3", PASS, 0, 2)
-        cast(nc.scalar.copy, "w3", PASS, 2, 4)
+        cast(nc.scalar.copy, "w3", PASS, 2, 4, 192)
         quantise_hidden(0, 0, 512, "raw_w1_768")
         quantise_weights("w3", 1, 0, 2)
         quantise_weights("w3", 1, 2, 4)
@@ -250,10 +251,10 @@ def tile_picked_depth_glu_sigmoid_srt_p_kernel(
         for n in range(8):
             if n + 2 < 8:
                 sigmoid_tile(1, n + 2)
-            if n == 0:
+            if n < 2:
                 nc.scalar.copy(
-                    out=grouped_w2[:].rearrange("p g (c i) j -> p g c j i", i=4),
-                    in_=raw_w2[:].rearrange("p g j (c i) -> p g c j i", i=4),
+                    out=grouped_w2[:, n].rearrange("p (c i) j -> p c j i", i=4),
+                    in_=raw_w2[:, n].rearrange("p j (c i) -> p c j i", i=4),
                 )
             gated_tile(1, n)
             if n == 1:

@@ -21,6 +21,7 @@ PACK = 4
 PASS = P * PACK
 TOK = 128
 CHUNK = 256
+W3_CUT = 192
 
 
 def tile_picked_depth_glu_sigmoid_srt_p_kernel(
@@ -44,8 +45,10 @@ def tile_picked_depth_glu_sigmoid_srt_p_kernel(
         nc.vector.memset(scale_window[:], 0)
         result = sb([P, T], F32, "result")
         nc.vector.memset(result[:], 0.0)
+        warm_in = sb([P, 1], F32, "warm_in")
+        nc.gpsimd.memset(warm_in[:], 0.0)
         warm = sb([P, 1], F32, "warm")
-        nc.scalar.activation(out=warm[:], in_=result[:, 0:1], func=SIGMOID)
+        nc.scalar.activation(out=warm[:], in_=warm_in[:], func=SIGMOID)
 
 
         raw = {}
@@ -61,8 +64,8 @@ def tile_picked_depth_glu_sigmoid_srt_p_kernel(
         for q in range(4):
             nc.sync.dma_start(out=scale_window[32 * q : 32 * q + 4, :], in_=scale_rows[4 * q : 4 * q + 4, :])
         load_first_layer("w1", w1, 256, PASS)
-        load_first_layer("w3", w3, 0, 192)
-        load_first_layer("w3", w3, 192, PASS)
+        load_first_layer("w3", w3, 0, W3_CUT)
+        load_first_layer("w3", w3, W3_CUT, PASS)
         word_window = sb([P, T], U32, "word_window")
         word_rows = x_words[0].rearrange("p n t -> p (n t)").bitcast(I32)
         cuts = [0, 160, 416, 672, S]
@@ -83,50 +86,53 @@ def tile_picked_depth_glu_sigmoid_srt_p_kernel(
         grouped, codes, scales = {}, {}, {}
         for name in ("w1", "w3"):
             for g in range(2):
-                if (name, g) != ("w1", 1):
+                if g == 0:
                     grouped[name, g] = sb([P, PACK, P, PACK], BF16, "grouped_%s_%d" % (name, g))
                 codes[name, g] = sb([P, PASS], U32, "codes_%s_%d" % (name, g))
                 scales[name, g] = sb([P, PASS], U8, "scales_%s_%d" % (name, g))
 
-        def cast(copy, name, lo, t_lo, t_hi, skip=0):
-            piece = raw[name, lo][:, :, skip:]
-            m_lo = (lo + skip) % PASS // PACK
-            words = grouped[name, lo // PASS][:, t_lo:t_hi, m_lo : m_lo + piece.shape[2] // PACK, :]
-            if lo >= PASS:
-                copy(
-                    out=words.rearrange("p t (a r) j -> p a j r t", r=2),
-                    in_=piece.rearrange("p j (a r t) -> p a j r t", t=PACK, r=2)[:, :, :, :, t_lo:t_hi],
-                )
-                return
+        def cast(copy, name, lo, t_lo, t_hi):
+            piece = raw[name, lo][:]
+            m_lo = lo % PASS // PACK
+            words = grouped[name, 0][:, t_lo:t_hi, m_lo : m_lo + piece.shape[2] // PACK, :]
             copy(
                 out=words.rearrange("p t (a r) j -> p a t j r", r=PACK),
                 in_=piece.rearrange("p j (a t r) -> p a t j r", t=PACK, r=PACK)[:, :, t_lo:t_hi],
             )
 
-        def cast_on_gpsimd(name, lo, t_lo, m_hi):
-            m_lo = lo % PASS // PACK
+        def cast_on_scalar(words, name, lo, t_lo, t_hi, m_lo, m_hi):
+            skip = lo % PASS // PACK
+            piece = raw[name, lo][:, :, (m_lo - skip) * PACK : (m_hi - skip) * PACK]
+            nc.scalar.copy(
+                out=words[:, :, m_lo:m_hi].rearrange("p t (a r) j -> p a j r t", r=2),
+                in_=piece.rearrange("p j (a r t) -> p a j r t", t=PACK, r=2)[:, :, :, :, t_lo:t_hi],
+            )
+
+        def cast_on_gpsimd(words, name, lo, t_lo, t_hi, m_lo, m_hi):
+            skip = lo % PASS // PACK
+            piece = raw[name, lo][:, :, (m_lo - skip) * PACK : (m_hi - skip) * PACK]
             nc.gpsimd.tensor_scalar(
-                out=grouped[name, 1][:, t_lo:, m_lo:m_hi, :].rearrange("p t m j -> p m t j"),
-                in0=raw[name, lo][:].rearrange("p j (m t) -> p m t j", t=PACK)[:, : m_hi - m_lo, t_lo:],
+                out=words[:, :, m_lo:m_hi].rearrange("p t m j -> p m t j"),
+                in0=piece.rearrange("p j (m t) -> p m t j", t=PACK)[:, :, t_lo:t_hi],
                 scalar1=1.0,
                 scalar2=0.0,
                 op0=MULT,
                 op1=ADD,
             )
 
-        def quantise_weights(name, g, t_lo, t_hi):
+        def quantise_weights(name, g, t_lo, t_hi, words):
             cols = slice(t_lo * P, t_hi * P)
             nc.vector.quantize_mx(
                 out=codes[name, g][:, cols].bitcast(FP8X4),
                 scales=scales[name, g][:, cols],
-                in_=grouped[name, g][:, t_lo:t_hi].rearrange("p t m j -> p (t m j)"),
+                in_=words.rearrange("p t m j -> p (t m j)"),
             )
 
         x_codes = sb([P, S], U32, "x_codes")
         x_bytes = sb([P, S], U8, "x_bytes")
 
-        def first_layer(name, g, n, bufs):
-            bank = psum.tile([P, PACK, TOK], F32, name="bank_" + name, tag="bank_" + name, bufs=bufs)
+        def first_layer(name, g, n, tag, bufs):
+            bank = psum.tile([P, PACK, TOK], F32, name="bank_" + name, tag=tag, bufs=bufs)
             toks = slice(n * TOK, (n + 1) * TOK)
             for t in range(PACK):
                 cols = slice(t * P, (t + 1) * P)
@@ -157,41 +163,77 @@ def tile_picked_depth_glu_sigmoid_srt_p_kernel(
         sig = {}
 
         def sigmoid_tile(g, n):
-            bank = first_layer("w1", g, n, 3)
+            bank = first_layer("w1", g, n, "bank_w1", 3)
             sig[g, n] = sb([P, TOK, PACK], F32, "sig_%d_%d" % (g, n))
             nc.scalar.activation(out=sig[g, n][:], in_=bank[:].rearrange("p t n -> p n t"), func=SIGMOID)
 
-        hidden = [sb([P, S, PACK], BF16, "hidden_%d" % g) for g in range(2)]
+        hidden = {}
+
+        def hidden_words(g, lo, hi):
+            width = PASS if g == 0 else CHUNK if lo < S - CHUNK else TOK
+            first = lo // width * width
+            if (g, first) not in hidden:
+                tag = "hidden_1_0" if (g, first) == (1, CHUNK) else None
+                hidden[g, first] = sb([P, width, PACK], BF16, "hidden_%d_%d" % (g, first), tag)
+            return hidden[g, first][:, lo - first : hi - first, :]
+
         h_codes = {}
         h_scales = [sb([P, S], U8, "h_scales_%d" % g) for g in range(2)]
 
-        def gated_tile(g, n):
-            bank = first_layer("w3", g, n, 3)
+        def gated_tile(g, n, tag="bank_w3", bufs=3):
+            bank = first_layer("w3", g, n, tag, bufs)
             nc.vector.tensor_tensor(
-                out=hidden[g][:, n * TOK : (n + 1) * TOK, :],
+                out=hidden_words(g, n * TOK, (n + 1) * TOK),
                 in0=bank[:].rearrange("p t n -> p n t"),
                 in1=sig[g, n][:],
                 op=MULT,
             )
 
+        linear = {}
+
+        def empty_bank(g, n):
+            bank = first_layer("w3", g, n, "bank_w3", 3)
+            linear[g, n] = sb([P, TOK, PACK], F32, "linear_%d_%d" % (g, n))
+            nc.scalar.copy(out=linear[g, n][:], in_=bank[:].rearrange("p t n -> p n t"))
+
+        def gated_tile_on_gpsimd(g, n):
+            nc.gpsimd.tensor_tensor(
+                out=hidden_words(g, n * TOK, (n + 1) * TOK), in0=linear[g, n][:], in1=sig[g, n][:], op=MULT
+            )
+
         def hidden_codes(g, lo, hi):
-            width = PASS if g == 0 else CHUNK
-            return h_codes[g, lo // width][:, lo % width : lo % width + hi - lo].bitcast(FP8X4)
+            start = max(first for half, first in h_codes if half == g and first <= lo)
+            return h_codes[g, start][:, lo - start : hi - start].bitcast(FP8X4)
 
         def quantise_hidden(g, lo, hi, tag=None):
-            width = PASS if g == 0 else CHUNK
-            if lo % width == 0:
-                h_codes[g, lo // width] = sb([P, width], U32, "h_codes_%d_%d" % (g, lo), tag)
+            h_codes[g, lo] = sb([P, hi - lo], U32, "h_codes_%d_%d" % (g, lo), tag)
             nc.vector.quantize_mx(
                 out=hidden_codes(g, lo, hi),
                 scales=h_scales[g][:, lo:hi],
-                in_=hidden[g][:, lo:hi, :].rearrange("p n t -> p (n t)"),
+                in_=hidden_words(g, lo, hi).rearrange("p n t -> p (n t)"),
             )
 
-        grouped_w2 = sb([P, 2, N, PACK], BF16, "grouped_w2")
         w2_codes = sb([P, 2 * N], U32, "w2_codes")
         w2_scales = sb([P, 2 * N], U8, "w2_scales")
-        y = sb([P, S], F32, "y")
+        y = [sb([P, CHUNK], F32, "y_%d" % c) for c in range(S // CHUNK)]
+
+        def cast_w2():
+            grouped["w2"] = sb([P, 2, N, PACK], BF16, "grouped_w2", "hidden_0_512")
+            nc.gpsimd.tensor_scalar(
+                out=grouped["w2"][:],
+                in0=raw_w2[:].rearrange("p g j n -> p g n j"),
+                scalar1=1.0,
+                scalar2=0.0,
+                op0=MULT,
+                op1=ADD,
+            )
+
+        def quantise_w2():
+            nc.vector.quantize_mx(
+                out=w2_codes[:].bitcast(FP8X4),
+                scales=w2_scales[:],
+                in_=grouped["w2"][:].rearrange("p g n j -> p (g n j)"),
+            )
 
         def second_layer(lo, hi):
             toks = slice(lo, hi)
@@ -207,75 +249,81 @@ def tile_picked_depth_glu_sigmoid_srt_p_kernel(
                     start=(g == 0),
                     stop=(g == 1),
                 )
-            nc.scalar.copy(out=y[:, toks], in_=bank[:])
+            nc.scalar.copy(out=y[lo // CHUNK][:, lo % CHUNK : lo % CHUNK + hi - lo], in_=bank[:])
 
-        def scatter(c):
-            lo, hi = c * CHUNK, (c + 1) * CHUNK
-            nc.vector.tensor_tensor(result[:].indirect(entries(lo, hi)), y[:, lo:hi], gates[:, lo:hi], MULT)
+        def scatter(lo, hi):
+            nc.vector.tensor_tensor(result[:].indirect(entries(lo, hi)), y[lo // CHUNK][:], gates[:, lo:hi], MULT)
+
+        def gather_words(c):
+            lo, hi = cuts[c], cuts[c + 1]
+            nc.vector.tensor_copy(x_codes[:, lo:hi], word_window[:, : reach[c]].indirect(entries(lo, hi)))
 
         nc.vector.tensor_copy(x_bytes[:], scale_window[:].bitcast(U8).indirect(offsets[:]))
         cast(nc.scalar.copy, "w1", 0, 0, PACK)
         cast(nc.scalar.copy, "w1", 256, 0, PACK)
         cast(nc.vector.tensor_copy, "w3", 0, 0, 2)
-        quantise_weights("w1", 0, 0, PACK)
+        quantise_weights("w1", 0, 0, PACK, grouped["w1", 0][:])
         keep_clock("bank_y", 2, 3)
         cast(nc.scalar.copy, "w3", 0, 2, PACK)
-        cast(nc.scalar.copy, "w3", 192, 2, PACK)
-        cast(nc.vector.tensor_copy, "w3", 192, 0, 2)
-        quantise_weights("w3", 0, 0, 2)
-        quantise_weights("w3", 0, 2, PACK)
+        cast(nc.scalar.copy, "w3", W3_CUT, 2, PACK)
+        cast(nc.vector.tensor_copy, "w3", W3_CUT, 0, 2)
+        quantise_weights("w3", 0, 0, 2, grouped["w3", 0][:, :2])
+        quantise_weights("w3", 0, 2, PACK, grouped["w3", 0][:, 2:])
         for c in range(4):
-            lo, hi = cuts[c], cuts[c + 1]
-            nc.vector.tensor_copy(x_codes[:, lo:hi], word_window[:, : reach[c]].indirect(entries(lo, hi)))
+            gather_words(c)
         for n in range(2):
             sigmoid_tile(0, n)
-        grouped["w1", 1] = sb([P, PACK, P, PACK], BF16, "grouped_w1_1", "word_window")
-        cast_on_gpsimd("w1", PASS, 0, P // 2)
-        cast_on_gpsimd("w1", PASS + PASS // 2, 0, P)
-        cast_on_gpsimd("w3", PASS, 2, 48)
+        w1_words = sb([P, PACK, P, PACK], BF16, "grouped_w1_1", "word_window")
+        w3_low = sb([P, 2, P, PACK], BF16, "grouped_w3_1_low")
+        w3_high = sb([P, 2, P, PACK], BF16, "grouped_w3_1_high")
+        cast_on_gpsimd(w1_words[:], "w1", PASS, 0, PACK, 0, 64)
+        cast_on_gpsimd(w1_words[:], "w1", PASS + PASS // 2, 0, PACK, 64, P)
+        cast_on_gpsimd(w3_high[:], "w3", PASS, 2, PACK, 0, 48)
         for n in range(8):
             gated_tile(0, n)
             if n + 2 < 8:
                 sigmoid_tile(0, n + 2)
-        quantise_weights("w1", 1, 0, PACK)
-        cast(nc.scalar.copy, "w3", PASS, 0, 2)
-        cast(nc.scalar.copy, "w3", PASS, 2, 4, 192)
+        quantise_weights("w1", 1, 0, PACK, w1_words[:])
+        cast_on_scalar(w3_low[:], "w3", PASS, 0, 2, 0, P)
+        cast_on_scalar(w3_high[:], "w3", PASS, 2, PACK, 48, P)
         quantise_hidden(0, 0, 512, "raw_w1_768")
-        quantise_weights("w3", 1, 0, 2)
-        quantise_weights("w3", 1, 2, 4)
+        quantise_weights("w3", 1, 0, 2, w3_low[:])
+        quantise_weights("w3", 1, 2, 4, w3_high[:])
         for i in range(3):
             keep_clock("bank_w3", 3, 1)
         sigmoid_tile(1, 0)
         sigmoid_tile(1, 1)
         quantise_hidden(0, 512, 1024, "raw_w3_512")
-        for n in range(8):
-            if n + 2 < 8:
-                sigmoid_tile(1, n + 2)
-            if n < 2:
-                nc.scalar.copy(
-                    out=grouped_w2[:, n].rearrange("p (c i) j -> p c j i", i=4),
-                    in_=raw_w2[:, n].rearrange("p j (c i) -> p c j i", i=4),
-                )
+        cast_w2()
+        sigmoid_tile(1, 4)
+        for n in (0, 1, 4):
             gated_tile(1, n)
-            if n == 1:
-                nc.vector.quantize_mx(
-                    out=w2_codes[:].bitcast(FP8X4),
-                    scales=w2_scales[:],
-                    in_=grouped_w2[:].rearrange("p g n j -> p (g n j)"),
-                )
-            if n >= 2 and n % 2 == 0:
-                lo = (n - 2) * TOK
-                quantise_hidden(1, lo, lo + CHUNK)
-                second_layer(lo, lo + CHUNK)
-            if n >= 4 and n % 2 == 0:
-                scatter(n // 2 - 2)
-            if n == 6:
-                settled = sb([P, 2 * CHUNK], F32, "settled", "h_codes_1_512")
-                nc.scalar.copy(out=settled[:], in_=result[:, : 2 * CHUNK])
-                nc.sync.dma_start(out=out[:, : 2 * CHUNK], in_=settled[:])
-        for n in (6, 7):
-            quantise_hidden(1, n * TOK, (n + 1) * TOK)
-            second_layer(n * TOK, (n + 1) * TOK)
-        scatter(2)
-        scatter(3)
+        sigmoid_tile(1, 2)
+        empty_bank(1, 2)
+        sigmoid_tile(1, 5)
+        sigmoid_tile(1, 3)
+        sigmoid_tile(1, 6)
+        quantise_w2()
+        quantise_hidden(1, 0, 256)
+        gated_tile_on_gpsimd(1, 2)
+        for n in (5, 3, 6):
+            gated_tile(1, n)
+        second_layer(0, 256)
+        sigmoid_tile(1, 7)
+        quantise_hidden(1, 256, 512)
+        second_layer(256, 512)
+        scatter(0, 256)
+        quantise_hidden(1, 512, 768)
+        second_layer(512, 768)
+        quantise_hidden(1, 768, 896)
+        scatter(256, 512)
+        settled = sb([P, 2 * CHUNK], F32, "settled")
+        nc.scalar.copy(out=settled[:], in_=result[:, : 2 * CHUNK])
+        nc.sync.dma_start(out=out[:, : 2 * CHUNK], in_=settled[:])
+        gated_tile(1, 7, "bank_y", 2)
+        second_layer(768, 896)
+        quantise_hidden(1, 896, S)
+        second_layer(896, S)
+        scatter(512, 768)
+        scatter(768, S)
         nc.sync.dma_start(out=out[:, 2 * CHUNK :], in_=result[:, 2 * CHUNK :])

@@ -21,6 +21,7 @@ PACK = 4
 PASS = P * PACK
 TOK = 128
 CHUNK = 256
+ON_GPSIMD = 64
 W3_CUT = 192
 
 
@@ -45,10 +46,8 @@ def tile_picked_depth_glu_sigmoid_srt_p_kernel(
         nc.vector.memset(scale_window[:], 0)
         result = sb([P, T], F32, "result")
         nc.vector.memset(result[:], 0.0)
-        warm_in = sb([P, 1], F32, "warm_in")
-        nc.gpsimd.memset(warm_in[:], 0.0)
         warm = sb([P, 1], F32, "warm")
-        nc.scalar.activation(out=warm[:], in_=warm_in[:], func=SIGMOID)
+        nc.scalar.activation(out=warm[:], in_=result[:, 0:1], func=SIGMOID)
 
 
         raw = {}
@@ -147,15 +146,15 @@ def tile_picked_depth_glu_sigmoid_srt_p_kernel(
                 )
             return bank
 
-        def keep_clock(tag, bufs, passes):
-            bank = psum.tile([P, PASS], F32, name=tag, tag=tag, bufs=bufs)
+        def keep_clock(tag, bufs, passes, width=PASS):
+            bank = psum.tile([P, width], F32, name=tag, tag=tag, bufs=bufs)
             for i in range(passes):
                 nc.tensor.matmul_mx(
                     out=bank[:],
                     lhsT=codes["w1", 0][:, :P].bitcast(FP8X4),
                     lhsT_scale=scales["w1", 0][:, :P],
-                    rhs=codes["w1", 0][:].bitcast(FP8X4),
-                    rhs_scale=scales["w1", 0][:],
+                    rhs=codes["w1", 0][:, :width].bitcast(FP8X4),
+                    rhs_scale=scales["w1", 0][:, :width],
                     start=True,
                     stop=True,
                 )
@@ -173,15 +172,15 @@ def tile_picked_depth_glu_sigmoid_srt_p_kernel(
             width = PASS if g == 0 else CHUNK if lo < S - CHUNK else TOK
             first = lo // width * width
             if (g, first) not in hidden:
-                tag = "hidden_1_0" if (g, first) == (1, CHUNK) else None
+                tag = "hidden_1_256" if (g, first) in ((1, 2 * CHUNK), (1, S - TOK)) else None
                 hidden[g, first] = sb([P, width, PACK], BF16, "hidden_%d_%d" % (g, first), tag)
             return hidden[g, first][:, lo - first : hi - first, :]
 
         h_codes = {}
         h_scales = [sb([P, S], U8, "h_scales_%d" % g) for g in range(2)]
 
-        def gated_tile(g, n, tag="bank_w3", bufs=3):
-            bank = first_layer("w3", g, n, tag, bufs)
+        def gated_tile(g, n):
+            bank = first_layer("w3", g, n, "bank_w3", 3)
             nc.vector.tensor_tensor(
                 out=hidden_words(g, n * TOK, (n + 1) * TOK),
                 in0=bank[:].rearrange("p t n -> p n t"),
@@ -189,16 +188,26 @@ def tile_picked_depth_glu_sigmoid_srt_p_kernel(
                 op=MULT,
             )
 
-        linear = {}
+        def shared_tile_begin(n):
+            bank = first_layer("w3", 1, n, "bank_w3", 3)
+            linear = sb([P, ON_GPSIMD, PACK], F32, "linear")
+            nc.scalar.copy(out=linear[:], in_=bank[:, :, :ON_GPSIMD].rearrange("p t n -> p n t"))
+            return bank, linear
 
-        def empty_bank(g, n):
-            bank = first_layer("w3", g, n, "bank_w3", 3)
-            linear[g, n] = sb([P, TOK, PACK], F32, "linear_%d_%d" % (g, n))
-            nc.scalar.copy(out=linear[g, n][:], in_=bank[:].rearrange("p t n -> p n t"))
-
-        def gated_tile_on_gpsimd(g, n):
+        def shared_tile_on_gpsimd(n, linear):
             nc.gpsimd.tensor_tensor(
-                out=hidden_words(g, n * TOK, (n + 1) * TOK), in0=linear[g, n][:], in1=sig[g, n][:], op=MULT
+                out=hidden_words(1, n * TOK, n * TOK + ON_GPSIMD),
+                in0=linear[:],
+                in1=sig[1, n][:, :ON_GPSIMD],
+                op=MULT,
+            )
+
+        def shared_tile_on_vector(n, bank):
+            nc.vector.tensor_tensor(
+                out=hidden_words(1, n * TOK + ON_GPSIMD, (n + 1) * TOK),
+                in0=bank[:, :, ON_GPSIMD:].rearrange("p t n -> p n t"),
+                in1=sig[1, n][:, ON_GPSIMD:],
+                op=MULT,
             )
 
         def hidden_codes(g, lo, hi):
@@ -215,7 +224,7 @@ def tile_picked_depth_glu_sigmoid_srt_p_kernel(
 
         w2_codes = sb([P, 2 * N], U32, "w2_codes")
         w2_scales = sb([P, 2 * N], U8, "w2_scales")
-        y = [sb([P, CHUNK], F32, "y_%d" % c) for c in range(S // CHUNK)]
+        y = {}
 
         def cast_w2():
             grouped["w2"] = sb([P, 2, N, PACK], BF16, "grouped_w2", "hidden_0_512")
@@ -249,6 +258,8 @@ def tile_picked_depth_glu_sigmoid_srt_p_kernel(
                     start=(g == 0),
                     stop=(g == 1),
                 )
+            if lo % CHUNK == 0:
+                y[lo // CHUNK] = sb([P, CHUNK], F32, "y_%d" % (lo // CHUNK), "linear" if lo == CHUNK else None)
             nc.scalar.copy(out=y[lo // CHUNK][:, lo % CHUNK : lo % CHUNK + hi - lo], in_=bank[:])
 
         def scatter(lo, hi):
@@ -260,10 +271,12 @@ def tile_picked_depth_glu_sigmoid_srt_p_kernel(
 
         nc.vector.tensor_copy(x_bytes[:], scale_window[:].bitcast(U8).indirect(offsets[:]))
         cast(nc.scalar.copy, "w1", 0, 0, PACK)
-        cast(nc.scalar.copy, "w1", 256, 0, PACK)
+        cast(nc.scalar.copy, "w1", 256, 0, 2)
+        cast(nc.scalar.copy, "w1", 256, 2, PACK)
+        quantise_weights("w1", 0, 0, 2, grouped["w1", 0][:, :2])
+        keep_clock("bank_y", 2, 10, 256)
         cast(nc.vector.tensor_copy, "w3", 0, 0, 2)
-        quantise_weights("w1", 0, 0, PACK, grouped["w1", 0][:])
-        keep_clock("bank_y", 2, 3)
+        quantise_weights("w1", 0, 2, PACK, grouped["w1", 0][:, 2:])
         cast(nc.scalar.copy, "w3", 0, 2, PACK)
         cast(nc.scalar.copy, "w3", W3_CUT, 2, PACK)
         cast(nc.vector.tensor_copy, "w3", W3_CUT, 0, 2)
@@ -295,32 +308,32 @@ def tile_picked_depth_glu_sigmoid_srt_p_kernel(
         sigmoid_tile(1, 1)
         quantise_hidden(0, 512, 1024, "raw_w3_512")
         cast_w2()
-        sigmoid_tile(1, 4)
-        for n in (0, 1, 4):
+        for n in range(3):
+            sigmoid_tile(1, n + 2 if n < 2 else 5)
             gated_tile(1, n)
-        sigmoid_tile(1, 2)
-        empty_bank(1, 2)
-        sigmoid_tile(1, 5)
-        sigmoid_tile(1, 3)
+        quantise_hidden(1, 0, 256, "raw_w2")
+        gated_tile(1, 3)
+        bank, linear = shared_tile_begin(5)
         sigmoid_tile(1, 6)
+        sigmoid_tile(1, 4)
         quantise_w2()
-        quantise_hidden(1, 0, 256)
-        gated_tile_on_gpsimd(1, 2)
-        for n in (5, 3, 6):
-            gated_tile(1, n)
-        second_layer(0, 256)
-        sigmoid_tile(1, 7)
         quantise_hidden(1, 256, 512)
+        shared_tile_on_gpsimd(5, linear)
+        gated_tile(1, 6)
+        gated_tile(1, 4)
+        shared_tile_on_vector(5, bank)
+        second_layer(0, 256)
         second_layer(256, 512)
+        sigmoid_tile(1, 7)
         scatter(0, 256)
         quantise_hidden(1, 512, 768)
         second_layer(512, 768)
-        quantise_hidden(1, 768, 896)
         scatter(256, 512)
-        settled = sb([P, 2 * CHUNK], F32, "settled")
+        settled = sb([P, 2 * CHUNK], F32, "settled", "h_codes_1_512")
         nc.scalar.copy(out=settled[:], in_=result[:, : 2 * CHUNK])
         nc.sync.dma_start(out=out[:, : 2 * CHUNK], in_=settled[:])
-        gated_tile(1, 7, "bank_y", 2)
+        gated_tile(1, 7)
+        quantise_hidden(1, 768, 896, "linear")
         second_layer(768, 896)
         quantise_hidden(1, 896, S)
         second_layer(896, S)

@@ -73,7 +73,8 @@ def tile_picked_depth_glu_sigmoid_srt_p_kernel(
             nc.sync.dma_start(out=word_window[:, lo:hi].bitcast(I32), in_=word_rows[:, lo:hi])
         load_first_layer("w1", w1, PASS, PASS + PASS // 2)
         load_first_layer("w1", w1, PASS + PASS // 2, H)
-        load_first_layer("w3", w3, PASS, H)
+        load_first_layer("w3", w3, PASS, PASS + PASS // 2)
+        load_first_layer("w3", w3, PASS + PASS // 2, H)
         raw_w2 = sb([P, 2, PACK, N], F32, "raw_w2")
         w2_rows = w2[:PASS].rearrange("(a t r) n -> t a r n", t=PACK, r=PACK)
         for t in range(PACK):
@@ -99,10 +100,10 @@ def tile_picked_depth_glu_sigmoid_srt_p_kernel(
                 in_=piece.rearrange("p j (a t r) -> p a t j r", t=PACK, r=PACK)[:, :, t_lo:t_hi],
             )
 
-        def cast_on_scalar(words, name, lo, t_lo, t_hi, m_lo, m_hi):
+        def cast_on_scalar(words, name, lo, t_lo, t_hi, m_lo, m_hi, copy=nc.scalar.copy):
             skip = lo % PASS // PACK
             piece = raw[name, lo][:, :, (m_lo - skip) * PACK : (m_hi - skip) * PACK]
-            nc.scalar.copy(
+            copy(
                 out=words[:, :, m_lo:m_hi].rearrange("p t (a r) j -> p a j r t", r=2),
                 in_=piece.rearrange("p j (a r t) -> p a j r t", t=PACK, r=2)[:, :, :, :, t_lo:t_hi],
             )
@@ -172,7 +173,11 @@ def tile_picked_depth_glu_sigmoid_srt_p_kernel(
             width = PASS if g == 0 else CHUNK if lo < S - CHUNK else TOK
             first = lo // width * width
             if (g, first) not in hidden:
-                tag = "hidden_1_256" if (g, first) in ((1, 2 * CHUNK), (1, S - TOK)) else None
+                tag = None
+                if (g, first) in ((1, 2 * CHUNK), (1, S - TOK)):
+                    tag = "hidden_0_512"
+                if (g, first) == (1, S - CHUNK):
+                    tag = "hidden_1_0"
                 hidden[g, first] = sb([P, width, PACK], BF16, "hidden_%d_%d" % (g, first), tag)
             return hidden[g, first][:, lo - first : hi - first, :]
 
@@ -222,14 +227,17 @@ def tile_picked_depth_glu_sigmoid_srt_p_kernel(
                 in_=hidden_words(g, lo, hi).rearrange("p n t -> p (n t)"),
             )
 
-        w2_codes = sb([P, 2 * N], U32, "w2_codes")
-        w2_scales = sb([P, 2 * N], U8, "w2_scales")
+        joint_codes = sb([P, CHUNK + 2 * N], U32, "joint_codes")
+        joint_scales = sb([P, CHUNK + 2 * N], U8, "joint_scales")
+        w2_codes = joint_codes[:, CHUNK:]
+        w2_scales = joint_scales[:, CHUNK:]
         y = {}
 
         def cast_w2():
-            grouped["w2"] = sb([P, 2, N, PACK], BF16, "grouped_w2", "hidden_0_512")
+            grouped["joint"] = sb([P, CHUNK + 2 * N, PACK], BF16, "joint_words", "hidden_0_512")
+            hidden[1, CHUNK] = grouped["joint"][:, :CHUNK]
             nc.gpsimd.tensor_scalar(
-                out=grouped["w2"][:],
+                out=grouped["joint"][:, CHUNK:].rearrange("p (g n) j -> p g n j", g=2),
                 in0=raw_w2[:].rearrange("p g j n -> p g n j"),
                 scalar1=1.0,
                 scalar2=0.0,
@@ -237,11 +245,12 @@ def tile_picked_depth_glu_sigmoid_srt_p_kernel(
                 op1=ADD,
             )
 
-        def quantise_w2():
+        def quantise_joint():
+            h_codes[1, CHUNK] = joint_codes[:, :CHUNK]
             nc.vector.quantize_mx(
-                out=w2_codes[:].bitcast(FP8X4),
-                scales=w2_scales[:],
-                in_=grouped["w2"][:].rearrange("p g n j -> p (g n j)"),
+                out=joint_codes[:].bitcast(FP8X4),
+                scales=joint_scales[:],
+                in_=grouped["joint"][:].rearrange("p n j -> p (n j)"),
             )
 
         def second_layer(lo, hi):
@@ -254,7 +263,7 @@ def tile_picked_depth_glu_sigmoid_srt_p_kernel(
                     lhsT=w2_codes[:, cols].bitcast(FP8X4),
                     lhsT_scale=w2_scales[:, cols],
                     rhs=hidden_codes(g, lo, hi),
-                    rhs_scale=h_scales[g][:, toks],
+                    rhs_scale=joint_scales[:, :CHUNK] if (g, lo) == (1, CHUNK) else h_scales[g][:, toks],
                     start=(g == 0),
                     stop=(g == 1),
                 )
@@ -291,22 +300,23 @@ def tile_picked_depth_glu_sigmoid_srt_p_kernel(
         w3_high = sb([P, 2, P, PACK], BF16, "grouped_w3_1_high")
         cast_on_gpsimd(w1_words[:], "w1", PASS, 0, PACK, 0, 64)
         cast_on_gpsimd(w1_words[:], "w1", PASS + PASS // 2, 0, PACK, 64, P)
-        cast_on_gpsimd(w3_high[:], "w3", PASS, 2, PACK, 0, 48)
+        cast_on_gpsimd(w3_high[:], "w3", PASS, 2, PACK, 0, 64)
         for n in range(8):
             gated_tile(0, n)
             if n + 2 < 8:
                 sigmoid_tile(0, n + 2)
         quantise_weights("w1", 1, 0, PACK, w1_words[:])
-        cast_on_scalar(w3_low[:], "w3", PASS, 0, 2, 0, P)
-        cast_on_scalar(w3_high[:], "w3", PASS, 2, PACK, 48, P)
+        cast_on_scalar(w3_low[:], "w3", PASS, 0, 2, 0, 64)
+        cast_on_scalar(w3_low[:], "w3", PASS + PASS // 2, 0, 2, 64, P)
         quantise_hidden(0, 0, 512, "raw_w1_768")
+        cast_on_scalar(w3_high[:], "w3", PASS + PASS // 2, 2, PACK, 64, P, nc.scalar.copy)
         quantise_weights("w3", 1, 0, 2, w3_low[:])
         quantise_weights("w3", 1, 2, 4, w3_high[:])
         for i in range(3):
             keep_clock("bank_w3", 3, 1)
         sigmoid_tile(1, 0)
         sigmoid_tile(1, 1)
-        quantise_hidden(0, 512, 1024, "raw_w3_512")
+        quantise_hidden(0, 512, 1024, "raw_w3_768")
         cast_w2()
         for n in range(3):
             sigmoid_tile(1, n + 2 if n < 2 else 5)
@@ -316,8 +326,7 @@ def tile_picked_depth_glu_sigmoid_srt_p_kernel(
         bank, linear = shared_tile_begin(5)
         sigmoid_tile(1, 6)
         sigmoid_tile(1, 4)
-        quantise_w2()
-        quantise_hidden(1, 256, 512)
+        quantise_joint()
         shared_tile_on_gpsimd(5, linear)
         gated_tile(1, 6)
         gated_tile(1, 4)

@@ -296,17 +296,17 @@ def tile_picked_depth_glu_sigmoid_srt_p_kernel(
         for n in range(2):
             sigmoid_tile(0, n)
         w1_words = sb([P, PACK, P, PACK], BF16, "grouped_w1_1", "word_window")
-        w3_low = sb([P, 2, P, PACK], BF16, "grouped_w3_1_low")
-        w3_high = sb([P, 2, P, PACK], BF16, "grouped_w3_1_high")
         cast_on_gpsimd(w1_words[:], "w1", PASS, 0, PACK, 0, 64)
         cast_on_gpsimd(w1_words[:], "w1", PASS + PASS // 2, 0, PACK, 64, P)
-        cast_on_gpsimd(w3_high[:], "w3", PASS, 2, PACK, 0, 64)
         for n in range(8):
             gated_tile(0, n)
             if n + 2 < 8:
                 sigmoid_tile(0, n + 2)
         quantise_weights("w1", 1, 0, PACK, w1_words[:])
+        w3_low = sb([P, 2, P, PACK], BF16, "grouped_w3_1_low", "sig_0_4")
+        w3_high = sb([P, 2, P, PACK], BF16, "grouped_w3_1_high", "sig_0_3")
         cast_on_scalar(w3_low[:], "w3", PASS, 0, 2, 0, 64)
+        cast_on_scalar(w3_high[:], "w3", PASS, 2, PACK, 0, 64)
         cast_on_scalar(w3_low[:], "w3", PASS + PASS // 2, 0, 2, 64, P)
         quantise_hidden(0, 0, 512, "raw_w1_768")
         cast_on_scalar(w3_high[:], "w3", PASS + PASS // 2, 2, PACK, 64, P, nc.scalar.copy)

@@ -67,14 +67,14 @@ def tile_picked_depth_glu_sigmoid_srt_p_kernel(
         load_first_layer("w3", w3, W3_CUT, PASS)
         word_window = sb([P, T], U32, "word_window")
         word_rows = x_words[0].rearrange("p n t -> p (n t)").bitcast(I32)
-        cuts = [0, 160, 416, 672, S]
+        cuts = [0, 160, 512, S]
         reach = [T - S + hi for hi in cuts[1:]]
-        for lo, hi in ((0, reach[0]), (reach[0], reach[1]), (reach[1], T)):
+        for lo, hi in zip([0] + reach, reach):
             nc.sync.dma_start(out=word_window[:, lo:hi].bitcast(I32), in_=word_rows[:, lo:hi])
         load_first_layer("w1", w1, PASS, PASS + PASS // 2)
         load_first_layer("w1", w1, PASS + PASS // 2, H)
-        load_first_layer("w3", w3, PASS, PASS + PASS // 2)
-        load_first_layer("w3", w3, PASS + PASS // 2, H)
+        load_first_layer("w3", w3, PASS, PASS + 320)
+        load_first_layer("w3", w3, PASS + 320, H)
         raw_w2 = sb([P, 2, PACK, N], F32, "raw_w2")
         w2_rows = w2[:PASS].rearrange("(a t r) n -> t a r n", t=PACK, r=PACK)
         for t in range(PACK):
@@ -88,7 +88,8 @@ def tile_picked_depth_glu_sigmoid_srt_p_kernel(
             for g in range(2):
                 if g == 0:
                     grouped[name, g] = sb([P, PACK, P, PACK], BF16, "grouped_%s_%d" % (name, g))
-                codes[name, g] = sb([P, PASS], U32, "codes_%s_%d" % (name, g))
+                if (name, g) != ("w1", 1):
+                    codes[name, g] = sb([P, PASS], U32, "codes_%s_%d" % (name, g))
                 scales[name, g] = sb([P, PASS], U8, "scales_%s_%d" % (name, g))
 
         def cast(copy, name, lo, t_lo, t_hi):
@@ -291,32 +292,34 @@ def tile_picked_depth_glu_sigmoid_srt_p_kernel(
         cast(nc.vector.tensor_copy, "w3", W3_CUT, 0, 2)
         quantise_weights("w3", 0, 0, 2, grouped["w3", 0][:, :2])
         quantise_weights("w3", 0, 2, PACK, grouped["w3", 0][:, 2:])
-        for c in range(4):
+        for c in range(len(reach)):
             gather_words(c)
         for n in range(2):
             sigmoid_tile(0, n)
         w1_words = sb([P, PACK, P, PACK], BF16, "grouped_w1_1", "word_window")
         cast_on_gpsimd(w1_words[:], "w1", PASS, 0, PACK, 0, 64)
         cast_on_gpsimd(w1_words[:], "w1", PASS + PASS // 2, 0, PACK, 64, P)
+        w3_high = sb([P, 2, P, PACK], BF16, "grouped_w3_1_high")
+        cast_on_gpsimd(w3_high[:], "w3", PASS, 2, PACK, 0, 48)
         for n in range(8):
             gated_tile(0, n)
             if n + 2 < 8:
                 sigmoid_tile(0, n + 2)
+        codes["w1", 1] = sb([P, PASS], U32, "codes_w1_1", "sig_0_6")
         quantise_weights("w1", 1, 0, PACK, w1_words[:])
         w3_low = sb([P, 2, P, PACK], BF16, "grouped_w3_1_low", "sig_0_4")
-        w3_high = sb([P, 2, P, PACK], BF16, "grouped_w3_1_high", "sig_0_3")
-        cast_on_scalar(w3_low[:], "w3", PASS, 0, 2, 0, 64)
-        cast_on_scalar(w3_high[:], "w3", PASS, 2, PACK, 0, 64)
-        cast_on_scalar(w3_low[:], "w3", PASS + PASS // 2, 0, 2, 64, P)
-        quantise_hidden(0, 0, 512, "raw_w1_768")
-        cast_on_scalar(w3_high[:], "w3", PASS + PASS // 2, 2, PACK, 64, P, nc.scalar.copy)
+        cast_on_scalar(w3_low[:], "w3", PASS, 0, 2, 0, 80)
+        cast_on_scalar(w3_high[:], "w3", PASS, 2, PACK, 48, 80)
+        cast_on_scalar(w3_low[:], "w3", PASS + 320, 0, 2, 80, P)
+        quantise_hidden(0, 0, 512, "sig_0_7")
+        cast_on_scalar(w3_high[:], "w3", PASS + 320, 2, PACK, 80, P)
         quantise_weights("w3", 1, 0, 2, w3_low[:])
         quantise_weights("w3", 1, 2, 4, w3_high[:])
         for i in range(3):
             keep_clock("bank_w3", 3, 1)
         sigmoid_tile(1, 0)
         sigmoid_tile(1, 1)
-        quantise_hidden(0, 512, 1024, "raw_w3_768")
+        quantise_hidden(0, 512, 1024, "raw_w3_832")
         cast_w2()
         for n in range(3):
             sigmoid_tile(1, n + 2 if n < 2 else 5)

@@ -21,7 +21,7 @@ PACK = 4
 PASS = P * PACK
 TOK = 128
 CHUNK = 256
-ON_GPSIMD = 64
+ON_GPSIMD = 96
 W3_CUT = 192
 
 
@@ -163,9 +163,9 @@ def tile_picked_depth_glu_sigmoid_srt_p_kernel(
 
         sig = {}
 
-        def sigmoid_tile(g, n):
+        def sigmoid_tile(g, n, tag=None):
             bank = first_layer("w1", g, n, "bank_w1", 3)
-            sig[g, n] = sb([P, TOK, PACK], F32, "sig_%d_%d" % (g, n))
+            sig[g, n] = sb([P, TOK, PACK], F32, "sig_%d_%d" % (g, n), tag)
             nc.scalar.activation(out=sig[g, n][:], in_=bank[:].rearrange("p t n -> p n t"), func=SIGMOID)
 
         hidden = {}
@@ -269,7 +269,7 @@ def tile_picked_depth_glu_sigmoid_srt_p_kernel(
                     stop=(g == 1),
                 )
             if lo % CHUNK == 0:
-                y[lo // CHUNK] = sb([P, CHUNK], F32, "y_%d" % (lo // CHUNK), "linear" if lo == CHUNK else None)
+                y[lo // CHUNK] = sb([P, CHUNK], F32, "y_%d" % (lo // CHUNK), "linear" if lo == 0 else None)
             nc.scalar.copy(out=y[lo // CHUNK][:, lo % CHUNK : lo % CHUNK + hi - lo], in_=bank[:])
 
         def scatter(lo, hi):
@@ -314,33 +314,34 @@ def tile_picked_depth_glu_sigmoid_srt_p_kernel(
         quantise_hidden(0, 0, 512, "sig_0_7")
         cast_on_scalar(w3_high[:], "w3", PASS + 320, 2, PACK, 80, P)
         quantise_weights("w3", 1, 0, 2, w3_low[:])
-        quantise_weights("w3", 1, 2, 4, w3_high[:])
+        quantise_weights("w3", 1, 2, 3, w3_high[:, :1])
+        quantise_weights("w3", 1, 3, 4, w3_high[:, 1:])
         for i in range(3):
             keep_clock("bank_w3", 3, 1)
         sigmoid_tile(1, 0)
-        sigmoid_tile(1, 1)
+        sigmoid_tile(1, 2)
         quantise_hidden(0, 512, 1024, "raw_w3_832")
         cast_w2()
-        for n in range(3):
-            sigmoid_tile(1, n + 2 if n < 2 else 5)
+        for ahead, n in ((3, 0), (1, 2), (5, 3)):
+            sigmoid_tile(1, ahead)
             gated_tile(1, n)
-        quantise_hidden(1, 0, 256, "raw_w2")
-        gated_tile(1, 3)
+        sigmoid_tile(1, 4)
+        gated_tile(1, 1)
         bank, linear = shared_tile_begin(5)
         sigmoid_tile(1, 6)
-        sigmoid_tile(1, 4)
         quantise_joint()
+        quantise_hidden(1, 0, 256)
         shared_tile_on_gpsimd(5, linear)
-        gated_tile(1, 6)
         gated_tile(1, 4)
+        gated_tile(1, 6)
         shared_tile_on_vector(5, bank)
-        second_layer(0, 256)
         second_layer(256, 512)
-        sigmoid_tile(1, 7)
-        scatter(0, 256)
+        second_layer(0, 256)
+        sigmoid_tile(1, 7, "sig_1_6")
+        scatter(256, 512)
         quantise_hidden(1, 512, 768)
         second_layer(512, 768)
-        scatter(256, 512)
+        scatter(0, 256)
         settled = sb([P, 2 * CHUNK], F32, "settled", "h_codes_1_512")
         nc.scalar.copy(out=settled[:], in_=result[:, : 2 * CHUNK])
         nc.sync.dma_start(out=out[:, : 2 * CHUNK], in_=settled[:])

@@ -284,7 +284,7 @@ def tile_picked_depth_glu_sigmoid_srt_p_kernel(
         cast(nc.scalar.copy, "w1", 256, 0, 2)
         cast(nc.scalar.copy, "w1", 256, 2, PACK)
         quantise_weights("w1", 0, 0, 2, grouped["w1", 0][:, :2])
-        keep_clock("bank_y", 2, 10, 256)
+        keep_clock("bank_y", 2, 7, 256)
         cast(nc.vector.tensor_copy, "w3", 0, 0, 2)
         quantise_weights("w1", 0, 2, PACK, grouped["w1", 0][:, 2:])
         cast(nc.scalar.copy, "w3", 0, 2, PACK)

@@ -22,7 +22,7 @@ PASS = P * PACK
 TOK = 128
 CHUNK = 256
 ON_GPSIMD = 96
-W3_CUT = 192
+W3_CUT = 256
 
 
 def tile_picked_depth_glu_sigmoid_srt_p_kernel(
@@ -73,8 +73,8 @@ def tile_picked_depth_glu_sigmoid_srt_p_kernel(
             nc.sync.dma_start(out=word_window[:, lo:hi].bitcast(I32), in_=word_rows[:, lo:hi])
         load_first_layer("w1", w1, PASS, PASS + PASS // 2)
         load_first_layer("w1", w1, PASS + PASS // 2, H)
-        load_first_layer("w3", w3, PASS, PASS + 320)
-        load_first_layer("w3", w3, PASS + 320, H)
+        load_first_layer("w3", w3, PASS, PASS + 256)
+        load_first_layer("w3", w3, PASS + 256, H)
         raw_w2 = sb([P, 2, PACK, N], F32, "raw_w2")
         w2_rows = w2[:PASS].rearrange("(a t r) n -> t a r n", t=PACK, r=PACK)
         for t in range(PACK):
@@ -308,11 +308,11 @@ def tile_picked_depth_glu_sigmoid_srt_p_kernel(
         codes["w1", 1] = sb([P, PASS], U32, "codes_w1_1", "sig_0_6")
         quantise_weights("w1", 1, 0, PACK, w1_words[:])
         w3_low = sb([P, 2, P, PACK], BF16, "grouped_w3_1_low", "sig_0_4")
-        cast_on_scalar(w3_low[:], "w3", PASS, 0, 2, 0, 80)
-        cast_on_scalar(w3_high[:], "w3", PASS, 2, PACK, 48, 80)
-        cast_on_scalar(w3_low[:], "w3", PASS + 320, 0, 2, 80, P)
+        cast_on_scalar(w3_low[:], "w3", PASS, 0, 2, 0, 64)
+        cast_on_scalar(w3_high[:], "w3", PASS, 2, PACK, 48, 64)
+        cast_on_scalar(w3_low[:], "w3", PASS + 256, 0, 2, 64, P)
         quantise_hidden(0, 0, 512, "sig_0_7")
-        cast_on_scalar(w3_high[:], "w3", PASS + 320, 2, PACK, 80, P)
+        cast_on_scalar(w3_high[:], "w3", PASS + 256, 2, PACK, 64, P)
         quantise_weights("w3", 1, 0, 2, w3_low[:])
         quantise_weights("w3", 1, 2, 3, w3_high[:, :1])
         quantise_weights("w3", 1, 3, 4, w3_high[:, 1:])
@@ -320,7 +320,7 @@ def tile_picked_depth_glu_sigmoid_srt_p_kernel(
             keep_clock("bank_w3", 3, 1)
         sigmoid_tile(1, 0)
         sigmoid_tile(1, 2)
-        quantise_hidden(0, 512, 1024, "raw_w3_832")
+        quantise_hidden(0, 512, 1024, "raw_w3_768")
         cast_w2()
         for ahead, n in ((3, 0), (1, 2), (5, 3)):
             sigmoid_tile(1, ahead)

@@ -171,12 +171,14 @@ def tile_picked_depth_glu_sigmoid_srt_p_kernel(
         hidden = {}
 
         def hidden_words(g, lo, hi):
-            width = PASS if g == 0 else CHUNK if lo < S - CHUNK else TOK
+            width = CHUNK if g == 0 or lo < S - CHUNK else TOK
             first = lo // width * width
+            if g == 0 and CHUNK <= lo < 3 * CHUNK:
+                first, width = CHUNK, 2 * CHUNK
             if (g, first) not in hidden:
                 tag = None
                 if (g, first) in ((1, 2 * CHUNK), (1, S - TOK)):
-                    tag = "hidden_0_512"
+                    tag = "hidden_0_256"
                 if (g, first) == (1, S - CHUNK):
                     tag = "hidden_1_0"
                 hidden[g, first] = sb([P, width, PACK], BF16, "hidden_%d_%d" % (g, first), tag)
@@ -220,8 +222,8 @@ def tile_picked_depth_glu_sigmoid_srt_p_kernel(
             start = max(first for half, first in h_codes if half == g and first <= lo)
             return h_codes[g, start][:, lo - start : hi - start].bitcast(FP8X4)
 
-        def quantise_hidden(g, lo, hi, tag=None):
-            h_codes[g, lo] = sb([P, hi - lo], U32, "h_codes_%d_%d" % (g, lo), tag)
+        def quantise_hidden(g, lo, hi, tag=None, codes=None):
+            h_codes[g, lo] = sb([P, hi - lo], U32, "h_codes_%d_%d" % (g, lo), tag) if codes is None else codes
             nc.vector.quantize_mx(
                 out=hidden_codes(g, lo, hi),
                 scales=h_scales[g][:, lo:hi],
@@ -235,7 +237,7 @@ def tile_picked_depth_glu_sigmoid_srt_p_kernel(
         y = {}
 
         def cast_w2():
-            grouped["joint"] = sb([P, CHUNK + 2 * N, PACK], BF16, "joint_words", "hidden_0_512")
+            grouped["joint"] = sb([P, CHUNK + 2 * N, PACK], BF16, "joint_words", "hidden_0_256")
             hidden[1, CHUNK] = grouped["joint"][:, :CHUNK]
             nc.gpsimd.tensor_scalar(
                 out=grouped["joint"][:, CHUNK:].rearrange("p (g n) j -> p g n j", g=2),
@@ -300,18 +302,18 @@ def tile_picked_depth_glu_sigmoid_srt_p_kernel(
         cast_on_gpsimd(w1_words[:], "w1", PASS, 0, PACK, 0, 64)
         cast_on_gpsimd(w1_words[:], "w1", PASS + PASS // 2, 0, PACK, 64, P)
         w3_high = sb([P, 2, P, PACK], BF16, "grouped_w3_1_high")
-        cast_on_gpsimd(w3_high[:], "w3", PASS, 2, PACK, 0, 48)
+        cast_on_gpsimd(w3_high[:], "w3", PASS, 2, PACK, 0, 64)
         for n in range(8):
             gated_tile(0, n)
             if n + 2 < 8:
                 sigmoid_tile(0, n + 2)
         codes["w1", 1] = sb([P, PASS], U32, "codes_w1_1", "sig_0_6")
-        quantise_weights("w1", 1, 0, PACK, w1_words[:])
+        quantise_weights("w1", 1, 0, 2, w1_words[:, :2])
+        quantise_weights("w1", 1, 2, PACK, w1_words[:, 2:])
         w3_low = sb([P, 2, P, PACK], BF16, "grouped_w3_1_low", "sig_0_4")
         cast_on_scalar(w3_low[:], "w3", PASS, 0, 2, 0, 64)
-        cast_on_scalar(w3_high[:], "w3", PASS, 2, PACK, 48, 64)
         cast_on_scalar(w3_low[:], "w3", PASS + 256, 0, 2, 64, P)
-        quantise_hidden(0, 0, 512, "sig_0_7")
+        quantise_hidden(0, 0, 256, "sig_0_7")
         cast_on_scalar(w3_high[:], "w3", PASS + 256, 2, PACK, 64, P)
         quantise_weights("w3", 1, 0, 2, w3_low[:])
         quantise_weights("w3", 1, 2, 3, w3_high[:, :1])
@@ -320,13 +322,11 @@ def tile_picked_depth_glu_sigmoid_srt_p_kernel(
             keep_clock("bank_w3", 3, 1)
         sigmoid_tile(1, 0)
         sigmoid_tile(1, 2)
-        quantise_hidden(0, 512, 1024, "raw_w3_768")
+        quantise_hidden(0, 256, 768, "raw_w3_768")
         cast_w2()
-        for ahead, n in ((3, 0), (1, 2), (5, 3)):
-            sigmoid_tile(1, ahead)
+        for n, ahead in ((0, 3), (2, 1), (3, 5), (1, 4)):
             gated_tile(1, n)
-        sigmoid_tile(1, 4)
-        gated_tile(1, 1)
+            sigmoid_tile(1, ahead)
         bank, linear = shared_tile_begin(5)
         sigmoid_tile(1, 6)
         quantise_joint()
@@ -346,7 +346,9 @@ def tile_picked_depth_glu_sigmoid_srt_p_kernel(
         nc.scalar.copy(out=settled[:], in_=result[:, : 2 * CHUNK])
         nc.sync.dma_start(out=out[:, : 2 * CHUNK], in_=settled[:])
         gated_tile(1, 7)
-        quantise_hidden(1, 768, 896, "linear")
+        late_codes = sb([P, CHUNK + TOK], U32, "late_codes", "linear")
+        quantise_hidden(0, 768, S, codes=late_codes[:, :CHUNK])
+        quantise_hidden(1, 768, 896, codes=late_codes[:, CHUNK:])
         second_layer(768, 896)
         quantise_hidden(1, 896, S)
         second_layer(896, S)

@@ -71,8 +71,8 @@ def tile_picked_depth_glu_sigmoid_srt_p_kernel(
         reach = [T - S + hi for hi in cuts[1:]]
         for lo, hi in zip([0] + reach, reach):
             nc.sync.dma_start(out=word_window[:, lo:hi].bitcast(I32), in_=word_rows[:, lo:hi])
-        load_first_layer("w1", w1, PASS, PASS + PASS // 2)
-        load_first_layer("w1", w1, PASS + PASS // 2, H)
+        load_first_layer("w1", w1, PASS, PASS + 192)
+        load_first_layer("w1", w1, PASS + 192, H)
         load_first_layer("w3", w3, PASS, PASS + 256)
         load_first_layer("w3", w3, PASS + 256, H)
         raw_w2 = sb([P, 2, PACK, N], F32, "raw_w2")
@@ -298,9 +298,9 @@ def tile_picked_depth_glu_sigmoid_srt_p_kernel(
             gather_words(c)
         for n in range(2):
             sigmoid_tile(0, n)
-        w1_words = sb([P, PACK, P, PACK], BF16, "grouped_w1_1", "word_window")
-        cast_on_gpsimd(w1_words[:], "w1", PASS, 0, PACK, 0, 64)
-        cast_on_gpsimd(w1_words[:], "w1", PASS + PASS // 2, 0, PACK, 64, P)
+        w1_words = sb([P, PACK, P, PACK], BF16, "grouped_w1_1")
+        cast_on_gpsimd(w1_words[:], "w1", PASS, 0, PACK, 0, 48)
+        cast_on_gpsimd(w1_words[:], "w1", PASS + 192, 0, PACK, 48, P)
         w3_high = sb([P, 2, P, PACK], BF16, "grouped_w3_1_high")
         cast_on_gpsimd(w3_high[:], "w3", PASS, 2, PACK, 0, 64)
         for n in range(8):

@@ -132,7 +132,11 @@ def tile_picked_depth_glu_sigmoid_srt_p_kernel(
         x_codes = sb([P, S], U32, "x_codes")
         x_bytes = sb([P, S], U8, "x_bytes")
 
+        linear_banks = [[0, 1, 2, 0, 1, 2, 1, 2], [0, 0, 1, 2, 2, 1, 0, 1]]
+
         def first_layer(name, g, n, tag, bufs):
+            if name == "w3":
+                tag, bufs = "bank_w3_%d" % linear_banks[g][n], 1
             bank = psum.tile([P, PACK, TOK], F32, name="bank_" + name, tag=tag, bufs=bufs)
             toks = slice(n * TOK, (n + 1) * TOK)
             for t in range(PACK):
@@ -148,11 +152,11 @@ def tile_picked_depth_glu_sigmoid_srt_p_kernel(
                 )
             return bank
 
-        def keep_clock(tag, bufs, passes, width=PASS):
-            bank = psum.tile([P, width], F32, name=tag, tag=tag, bufs=bufs)
-            for i in range(passes):
+        def keep_clock(tag, bufs, widths):
+            bank = psum.tile([P, PASS], F32, name=tag, tag=tag, bufs=bufs)
+            for width in widths:
                 nc.tensor.matmul_mx(
-                    out=bank[:],
+                    out=bank[:, :width],
                     lhsT=codes["w1", 0][:, :P].bitcast(FP8X4),
                     lhsT_scale=scales["w1", 0][:, :P],
                     rhs=codes["w1", 0][:, :width].bitcast(FP8X4),
@@ -286,9 +290,9 @@ def tile_picked_depth_glu_sigmoid_srt_p_kernel(
         cast(nc.scalar.copy, "w1", 256, 0, 2)
         cast(nc.scalar.copy, "w1", 256, 2, PACK)
         quantise_weights("w1", 0, 0, 2, grouped["w1", 0][:, :2])
-        keep_clock("bank_y", 2, 7, 256)
         cast(nc.vector.tensor_copy, "w3", 0, 0, 2)
         quantise_weights("w1", 0, 2, PACK, grouped["w1", 0][:, 2:])
+        keep_clock("bank_y", 2, [PASS, PASS, CHUNK])
         cast(nc.scalar.copy, "w3", 0, 2, PACK)
         cast(nc.scalar.copy, "w3", W3_CUT, 2, PACK)
         cast(nc.vector.tensor_copy, "w3", W3_CUT, 0, 2)
@@ -318,8 +322,7 @@ def tile_picked_depth_glu_sigmoid_srt_p_kernel(
         quantise_weights("w3", 1, 0, 2, w3_low[:])
         quantise_weights("w3", 1, 2, 3, w3_high[:, :1])
         quantise_weights("w3", 1, 3, 4, w3_high[:, 1:])
-        for i in range(3):
-            keep_clock("bank_w3", 3, 1)
+        keep_clock("bank_w3_2", 1, [PASS])
         sigmoid_tile(1, 0)
         sigmoid_tile(1, 2)
         quantise_hidden(0, 256, 768, "raw_w3_768")

@@ -132,7 +132,7 @@ def tile_picked_depth_glu_sigmoid_srt_p_kernel(
         x_codes = sb([P, S], U32, "x_codes")
         x_bytes = sb([P, S], U8, "x_bytes")
 
-        linear_banks = [[0, 1, 2, 0, 1, 2, 1, 2], [0, 0, 1, 2, 2, 1, 0, 1]]
+        linear_banks = [[0, 1, 2, 0, 1, 2, 0, 1], [0, 0, 1, 2, 2, 1, 0, 1]]
 
         def first_layer(name, g, n, tag, bufs):
             if name == "w3":
@@ -152,13 +152,13 @@ def tile_picked_depth_glu_sigmoid_srt_p_kernel(
                 )
             return bank
 
-        def keep_clock(tag, bufs, widths):
+        def keep_clock(tag, bufs, widths, rows):
             bank = psum.tile([P, PASS], F32, name=tag, tag=tag, bufs=bufs)
             for width in widths:
                 nc.tensor.matmul_mx(
-                    out=bank[:, :width],
-                    lhsT=codes["w1", 0][:, :P].bitcast(FP8X4),
-                    lhsT_scale=scales["w1", 0][:, :P],
+                    out=bank[:rows, :width],
+                    lhsT=codes["w1", 0][:, :rows].bitcast(FP8X4),
+                    lhsT_scale=scales["w1", 0][:, :rows],
                     rhs=codes["w1", 0][:, :width].bitcast(FP8X4),
                     rhs_scale=scales["w1", 0][:, :width],
                     start=True,
@@ -290,9 +290,10 @@ def tile_picked_depth_glu_sigmoid_srt_p_kernel(
         cast(nc.scalar.copy, "w1", 256, 0, 2)
         cast(nc.scalar.copy, "w1", 256, 2, PACK)
         quantise_weights("w1", 0, 0, 2, grouped["w1", 0][:, :2])
+        keep_clock("bank_y", 2, [CHUNK, CHUNK], P)
         cast(nc.vector.tensor_copy, "w3", 0, 0, 2)
         quantise_weights("w1", 0, 2, PACK, grouped["w1", 0][:, 2:])
-        keep_clock("bank_y", 2, [PASS, PASS, CHUNK])
+        keep_clock("bank_y", 2, [PASS, PASS], P // 2)
         cast(nc.scalar.copy, "w3", 0, 2, PACK)
         cast(nc.scalar.copy, "w3", W3_CUT, 2, PACK)
         cast(nc.vector.tensor_copy, "w3", W3_CUT, 0, 2)
@@ -322,7 +323,8 @@ def tile_picked_depth_glu_sigmoid_srt_p_kernel(
         quantise_weights("w3", 1, 0, 2, w3_low[:])
         quantise_weights("w3", 1, 2, 3, w3_high[:, :1])
         quantise_weights("w3", 1, 3, 4, w3_high[:, 1:])
-        keep_clock("bank_w3_2", 1, [PASS])
+        keep_clock("bank_w3_0", 1, [PASS], P // 2)
+        keep_clock("bank_w3_1", 1, [PASS], P // 2)
         sigmoid_tile(1, 0)
         sigmoid_tile(1, 2)
         quantise_hidden(0, 256, 768, "raw_w3_768")

@@ -15,13 +15,13 @@ FP8X4 = mybir.dt.float8_e4m3fn_x4
 MULT = mybir.AluOpType.mult
 ADD = mybir.AluOpType.add
 SIGMOID = mybir.ActivationFunctionType.Sigmoid
+COPY = mybir.ActivationFunctionType.Copy
 
 P = 128
 PACK = 4
 PASS = P * PACK
 TOK = 128
 CHUNK = 256
-ON_GPSIMD = 96
 W3_CUT = 256
 
 
@@ -175,13 +175,13 @@ def tile_picked_depth_glu_sigmoid_srt_p_kernel(
         hidden = {}
 
         def hidden_words(g, lo, hi):
-            width = CHUNK if g == 0 or lo < S - CHUNK else TOK
+            width = CHUNK
             first = lo // width * width
             if g == 0 and CHUNK <= lo < 3 * CHUNK:
                 first, width = CHUNK, 2 * CHUNK
             if (g, first) not in hidden:
                 tag = None
-                if (g, first) in ((1, 2 * CHUNK), (1, S - TOK)):
+                if (g, first) == (1, 2 * CHUNK):
                     tag = "hidden_0_256"
                 if (g, first) == (1, S - CHUNK):
                     tag = "hidden_1_0"
@@ -200,26 +200,15 @@ def tile_picked_depth_glu_sigmoid_srt_p_kernel(
                 op=MULT,
             )
 
-        def shared_tile_begin(n):
+        def linear_tile(n):
             bank = first_layer("w3", 1, n, "bank_w3", 3)
-            linear = sb([P, ON_GPSIMD, PACK], F32, "linear")
-            nc.scalar.copy(out=linear[:], in_=bank[:, :, :ON_GPSIMD].rearrange("p t n -> p n t"))
-            return bank, linear
+            linear = sb([P, TOK, PACK], F32, "linear")
+            nc.scalar.copy(out=linear[:], in_=bank[:].rearrange("p t n -> p n t"))
+            return linear
 
-        def shared_tile_on_gpsimd(n, linear):
+        def gated_tile_on_gpsimd(n, linear):
             nc.gpsimd.tensor_tensor(
-                out=hidden_words(1, n * TOK, n * TOK + ON_GPSIMD),
-                in0=linear[:],
-                in1=sig[1, n][:, :ON_GPSIMD],
-                op=MULT,
-            )
-
-        def shared_tile_on_vector(n, bank):
-            nc.vector.tensor_tensor(
-                out=hidden_words(1, n * TOK + ON_GPSIMD, (n + 1) * TOK),
-                in0=bank[:, :, ON_GPSIMD:].rearrange("p t n -> p n t"),
-                in1=sig[1, n][:, ON_GPSIMD:],
-                op=MULT,
+                out=hidden_words(1, n * TOK, (n + 1) * TOK), in0=linear[:], in1=sig[1, n][:], op=MULT
             )
 
         def hidden_codes(g, lo, hi):
@@ -274,9 +263,18 @@ def tile_picked_depth_glu_sigmoid_srt_p_kernel(
                     start=(g == 0),
                     stop=(g == 1),
                 )
-            if lo % CHUNK == 0:
-                y[lo // CHUNK] = sb([P, CHUNK], F32, "y_%d" % (lo // CHUNK), "linear" if lo == 0 else None)
-            nc.scalar.copy(out=y[lo // CHUNK][:, lo % CHUNK : lo % CHUNK + hi - lo], in_=bank[:])
+            return bank
+
+        def copy_out(lo, hi, bank):
+            y[lo // CHUNK] = sb([P, CHUNK], F32, "y_%d" % (lo // CHUNK))
+            nc.scalar.copy(out=y[lo // CHUNK][:], in_=bank[:])
+
+        def weigh(lo, hi, bank):
+            y[lo // CHUNK] = sb([P, CHUNK], F32, "y_%d" % (lo // CHUNK))
+            nc.vector.tensor_tensor(out=y[lo // CHUNK][:], in0=bank[:], in1=gates[:, lo:hi], op=MULT)
+
+        def scatter_on_scalar(lo, hi):
+            nc.scalar.activation(out=result[:].indirect(entries(lo, hi)), in_=y[lo // CHUNK][:], func=COPY)
 
         def scatter(lo, hi):
             nc.vector.tensor_tensor(result[:].indirect(entries(lo, hi)), y[lo // CHUNK][:], gates[:, lo:hi], MULT)
@@ -332,31 +330,29 @@ def tile_picked_depth_glu_sigmoid_srt_p_kernel(
         for n, ahead in ((0, 3), (2, 1), (3, 5), (1, 4)):
             gated_tile(1, n)
             sigmoid_tile(1, ahead)
-        bank, linear = shared_tile_begin(5)
+        linear = linear_tile(5)
         sigmoid_tile(1, 6)
+        sigmoid_tile(1, 7)
         quantise_joint()
         quantise_hidden(1, 0, 256)
-        shared_tile_on_gpsimd(5, linear)
+        gated_tile_on_gpsimd(5, linear)
+        upper = second_layer(256, 512)
+        lower = second_layer(0, 256)
         gated_tile(1, 4)
+        weigh(256, 512, upper)
+        scatter_on_scalar(256, 512)
         gated_tile(1, 6)
-        shared_tile_on_vector(5, bank)
-        second_layer(256, 512)
-        second_layer(0, 256)
-        sigmoid_tile(1, 7, "sig_1_6")
-        scatter(256, 512)
-        quantise_hidden(1, 512, 768)
-        second_layer(512, 768)
-        scatter(0, 256)
-        settled = sb([P, 2 * CHUNK], F32, "settled", "h_codes_1_512")
-        nc.scalar.copy(out=settled[:], in_=result[:, : 2 * CHUNK])
-        nc.sync.dma_start(out=out[:, : 2 * CHUNK], in_=settled[:])
+        weigh(0, 256, lower)
+        scatter_on_scalar(0, 256)
         gated_tile(1, 7)
-        late_codes = sb([P, CHUNK + TOK], U32, "late_codes", "linear")
-        quantise_hidden(0, 768, S, codes=late_codes[:, :CHUNK])
-        quantise_hidden(1, 768, 896, codes=late_codes[:, CHUNK:])
-        second_layer(768, 896)
-        quantise_hidden(1, 896, S)
-        second_layer(896, S)
+        quantise_hidden(1, 512, 768)
+        copy_out(512, 768, second_layer(512, 768))
+        quantise_hidden(0, 768, S, "linear")
+        settled = sb([P, 2 * CHUNK], F32, "settled", "hidden_0_256")
+        nc.vector.tensor_copy(out=settled[:], in_=result[:, : 2 * CHUNK])
+        nc.sync.dma_start(out=out[:, : 2 * CHUNK], in_=settled[:])
+        quantise_hidden(1, 768, S, "sig_1_7")
+        copy_out(768, S, second_layer(768, S))
         scatter(512, 768)
         scatter(768, S)
         nc.sync.dma_start(out=out[:, 2 * CHUNK :], in_=result[:, 2 * CHUNK :])

@@ -348,11 +348,11 @@ def tile_picked_depth_glu_sigmoid_srt_p_kernel(
         quantise_hidden(1, 512, 768)
         copy_out(512, 768, second_layer(512, 768))
         quantise_hidden(0, 768, S, "linear")
+        quantise_hidden(1, 768, S, "sig_1_7")
+        copy_out(768, S, second_layer(768, S))
         settled = sb([P, 2 * CHUNK], F32, "settled", "hidden_0_256")
         nc.vector.tensor_copy(out=settled[:], in_=result[:, : 2 * CHUNK])
         nc.sync.dma_start(out=out[:, : 2 * CHUNK], in_=settled[:])
-        quantise_hidden(1, 768, S, "sig_1_7")
-        copy_out(768, S, second_layer(768, S))
         scatter(512, 768)
         scatter(768, S)
         nc.sync.dma_start(out=out[:, 2 * CHUNK :], in_=result[:, 2 * CHUNK :])

from contextlib import ExitStack

import concourse.mybir as mybir

K, T, S, H, N = 512, 2048, 1024, 1024, 128
FLOPS = 2 * S * (2 * K * H + H * N)

F32 = mybir.dt.float32
BF16 = mybir.dt.bfloat16
I32 = mybir.dt.int32
U32 = mybir.dt.uint32
U16 = mybir.dt.uint16
U8 = mybir.dt.uint8
FP8X4 = mybir.dt.float8_e4m3fn_x4
MULT = mybir.AluOpType.mult
ADD = mybir.AluOpType.add
SIGMOID = mybir.ActivationFunctionType.Sigmoid
COPY = mybir.ActivationFunctionType.Copy

P = 128
PACK = 4
PASS = P * PACK
TOK = 128
CHUNK = 256
W3_CUT = 256


def tile_picked_depth_glu_sigmoid_srt_p_kernel(
    tc, x_words, x_scales, w1, w3, w2, gate, offs, out
):
    nc = tc.nc
    with ExitStack() as ctx:
        lists = ctx.enter_context(tc.tile_pool(name="lists", bufs=1))
        keep = ctx.enter_context(tc.tile_pool(name="keep", bufs=1))
        psum = ctx.enter_context(tc.psum_pool(name="psum", bufs=1))

        def sb(shape, dtype, name, tag=None):
            return keep.tile(shape, dtype, name=name, tag=tag or name, align_bytes=64)

        offsets = lists.tile([P, S // 16], U16, name="offsets")

        def entries(lo, hi):
            return offsets[:, lo // 16 : hi // 16]

        scale_window = sb([P, T // 4], I32, "scale_window")
        nc.vector.memset(scale_window[:], 0)
        result = sb([P, T], F32, "result")
        nc.vector.memset(result[:], 0.0)
        warm = sb([P, 1], F32, "warm")
        nc.scalar.activation(out=warm[:], in_=result[:, 0:1], func=SIGMOID)


        raw = {}

        def load_first_layer(name, w, lo, hi):
            rows = w.rearrange("(p j) c -> p j c", j=PACK)
            raw[name, lo] = sb([P, PACK, hi - lo], F32, "raw_%s_%d" % (name, lo))
            nc.sync.dma_start(out=raw[name, lo][:], in_=rows[:, :, lo:hi])

        load_first_layer("w1", w1, 0, 256)
        nc.sync.dma_start(offsets[:], offs)
        scale_rows = x_scales[0].bitcast(I32)
        for q in range(4):
            nc.sync.dma_start(out=scale_window[32 * q : 32 * q + 4, :], in_=scale_rows[4 * q : 4 * q + 4, :])
        load_first_layer("w1", w1, 256, PASS)
        load_first_layer("w3", w3, 0, W3_CUT)
        load_first_layer("w3", w3, W3_CUT, PASS)
        word_window = sb([P, T], U32, "word_window")
        word_rows = x_words[0].rearrange("p n t -> p (n t)").bitcast(I32)
        cuts = [0, 160, 512, S]
        reach = [T - S + hi for hi in cuts[1:]]
        for lo, hi in zip([0] + reach, reach):
            nc.sync.dma_start(out=word_window[:, lo:hi].bitcast(I32), in_=word_rows[:, lo:hi])
        load_first_layer("w1", w1, PASS, PASS + 192)
        load_first_layer("w1", w1, PASS + 192, H)
        load_first_layer("w3", w3, PASS, PASS + 256)
        load_first_layer("w3", w3, PASS + 256, H)
        raw_w2 = sb([P, 2, PACK, N], F32, "raw_w2")
        w2_rows = w2[:PASS].rearrange("(a t r) n -> t a r n", t=PACK, r=PACK)
        for t in range(PACK):
            nc.sync.dma_start(out=raw_w2[:, 0, t, :], in_=w2_rows[t])
        nc.sync.dma_start(out=raw_w2[:, 1], in_=w2[PASS:].rearrange("(p j) n -> p j n", j=PACK))
        gates = sb([P, S], F32, "gates")
        nc.sync.dma_start(out=gates[:], in_=gate)

        grouped, codes, scales = {}, {}, {}
        for name in ("w1", "w3"):
            for g in range(2):
                if g == 0:
                    grouped[name, g] = sb([P, PACK, P, PACK], BF16, "grouped_%s_%d" % (name, g))
                if (name, g) != ("w1", 1):
                    codes[name, g] = sb([P, PASS], U32, "codes_%s_%d" % (name, g))
                scales[name, g] = sb([P, PASS], U8, "scales_%s_%d" % (name, g))

        def cast(copy, name, lo, t_lo, t_hi):
            piece = raw[name, lo][:]
            m_lo = lo % PASS // PACK
            words = grouped[name, 0][:, t_lo:t_hi, m_lo : m_lo + piece.shape[2] // PACK, :]
            copy(
                out=words.rearrange("p t (a r) j -> p a t j r", r=PACK),
                in_=piece.rearrange("p j (a t r) -> p a t j r", t=PACK, r=PACK)[:, :, t_lo:t_hi],
            )

        def cast_on_scalar(words, name, lo, t_lo, t_hi, m_lo, m_hi, copy=nc.scalar.copy):
            skip = lo % PASS // PACK
            piece = raw[name, lo][:, :, (m_lo - skip) * PACK : (m_hi - skip) * PACK]
            copy(
                out=words[:, :, m_lo:m_hi].rearrange("p t (a r) j -> p a j r t", r=2),
                in_=piece.rearrange("p j (a r t) -> p a j r t", t=PACK, r=2)[:, :, :, :, t_lo:t_hi],
            )

        def cast_on_gpsimd(words, name, lo, t_lo, t_hi, m_lo, m_hi):
            skip = lo % PASS // PACK
            piece = raw[name, lo][:, :, (m_lo - skip) * PACK : (m_hi - skip) * PACK]
            nc.gpsimd.tensor_scalar(
                out=words[:, :, m_lo:m_hi].rearrange("p t m j -> p m t j"),
                in0=piece.rearrange("p j (m t) -> p m t j", t=PACK)[:, :, t_lo:t_hi],
                scalar1=1.0,
                scalar2=0.0,
                op0=MULT,
                op1=ADD,
            )

        def quantise_weights(name, g, t_lo, t_hi, words):
            cols = slice(t_lo * P, t_hi * P)
            nc.vector.quantize_mx(
                out=codes[name, g][:, cols].bitcast(FP8X4),
                scales=scales[name, g][:, cols],
                in_=words.rearrange("p t m j -> p (t m j)"),
            )

        x_codes = sb([P, S], U32, "x_codes")
        x_bytes = sb([P, S], U8, "x_bytes")

        linear_banks = [[0, 1, 2, 0, 1, 2, 0, 1], [0, 0, 1, 2, 2, 1, 0, 1]]

        def first_layer(name, g, n, tag, bufs):
            if name == "w3":
                tag, bufs = "bank_w3_%d" % linear_banks[g][n], 1
            bank = psum.tile([P, PACK, TOK], F32, name="bank_" + name, tag=tag, bufs=bufs)
            toks = slice(n * TOK, (n + 1) * TOK)
            for t in range(PACK):
                cols = slice(t * P, (t + 1) * P)
                nc.tensor.matmul_mx(
                    out=bank[:, t, :],
                    lhsT=codes[name, g][:, cols].bitcast(FP8X4),
                    lhsT_scale=scales[name, g][:, cols],
                    rhs=x_codes[:, toks].bitcast(FP8X4),
                    rhs_scale=x_bytes[:, toks],
                    start=True,
                    stop=True,
                )
            return bank

        def keep_clock(tag, bufs, widths, rows):
            bank = psum.tile([P, PASS], F32, name=tag, tag=tag, bufs=bufs)
            for width in widths:
                nc.tensor.matmul_mx(
                    out=bank[:rows, :width],
                    lhsT=codes["w1", 0][:, :rows].bitcast(FP8X4),
                    lhsT_scale=scales["w1", 0][:, :rows],
                    rhs=codes["w1", 0][:, :width].bitcast(FP8X4),
                    rhs_scale=scales["w1", 0][:, :width],
                    start=True,
                    stop=True,
                )

        sig = {}

        def sigmoid_tile(g, n, tag=None):
            bank = first_layer("w1", g, n, "bank_w1", 3)
            sig[g, n] = sb([P, TOK, PACK], F32, "sig_%d_%d" % (g, n), tag)
            nc.scalar.activation(out=sig[g, n][:], in_=bank[:].rearrange("p t n -> p n t"), func=SIGMOID)

        hidden = {}

        def hidden_words(g, lo, hi):
            width = CHUNK
            first = lo // width * width
            if g == 0 and CHUNK <= lo < 3 * CHUNK:
                first, width = CHUNK, 2 * CHUNK
            if (g, first) not in hidden:
                tag = None
                if (g, first) == (1, 2 * CHUNK):
                    tag = "hidden_0_256"
                if (g, first) == (1, S - CHUNK):
                    tag = "hidden_1_0"
                hidden[g, first] = sb([P, width, PACK], BF16, "hidden_%d_%d" % (g, first), tag)
            return hidden[g, first][:, lo - first : hi - first, :]

        h_codes = {}
        h_scales = [sb([P, S], U8, "h_scales_%d" % g) for g in range(2)]

        def gated_tile(g, n):
            bank = first_layer("w3", g, n, "bank_w3", 3)
            nc.vector.tensor_tensor(
                out=hidden_words(g, n * TOK, (n + 1) * TOK),
                in0=bank[:].rearrange("p t n -> p n t"),
                in1=sig[g, n][:],
                op=MULT,
            )

        def linear_tile(n):
            bank = first_layer("w3", 1, n, "bank_w3", 3)
            linear = sb([P, TOK, PACK], F32, "linear")
            nc.scalar.copy(out=linear[:], in_=bank[:].rearrange("p t n -> p n t"))
            return linear

        def gated_tile_on_gpsimd(n, linear):
            nc.gpsimd.tensor_tensor(
                out=hidden_words(1, n * TOK, (n + 1) * TOK), in0=linear[:], in1=sig[1, n][:], op=MULT
            )

        def hidden_codes(g, lo, hi):
            start = max(first for half, first in h_codes if half == g and first <= lo)
            return h_codes[g, start][:, lo - start : hi - start].bitcast(FP8X4)

        def quantise_hidden(g, lo, hi, tag=None, codes=None):
            h_codes[g, lo] = sb([P, hi - lo], U32, "h_codes_%d_%d" % (g, lo), tag) if codes is None else codes
            nc.vector.quantize_mx(
                out=hidden_codes(g, lo, hi),
                scales=h_scales[g][:, lo:hi],
                in_=hidden_words(g, lo, hi).rearrange("p n t -> p (n t)"),
            )

        joint_codes = sb([P, CHUNK + 2 * N], U32, "joint_codes")
        joint_scales = sb([P, CHUNK + 2 * N], U8, "joint_scales")
        w2_codes = joint_codes[:, CHUNK:]
        w2_scales = joint_scales[:, CHUNK:]
        y = {}

        def cast_w2():
            grouped["joint"] = sb([P, CHUNK + 2 * N, PACK], BF16, "joint_words", "hidden_0_256")
            hidden[1, CHUNK] = grouped["joint"][:, :CHUNK]
            nc.gpsimd.tensor_scalar(
                out=grouped["joint"][:, CHUNK:].rearrange("p (g n) j -> p g n j", g=2),
                in0=raw_w2[:].rearrange("p g j n -> p g n j"),
                scalar1=1.0,
                scalar2=0.0,
                op0=MULT,
                op1=ADD,
            )

        def quantise_joint():
            h_codes[1, CHUNK] = joint_codes[:, :CHUNK]
            nc.vector.quantize_mx(
                out=joint_codes[:].bitcast(FP8X4),
                scales=joint_scales[:],
                in_=grouped["joint"][:].rearrange("p n j -> p (n j)"),
            )

        def second_layer(lo, hi):
            toks = slice(lo, hi)
            bank = psum.tile([P, hi - lo], F32, name="bank_y", tag="bank_y", bufs=2)
            for g in range(2):
                cols = slice(g * N, (g + 1) * N)
                nc.tensor.matmul_mx(
                    out=bank[:],
                    lhsT=w2_codes[:, cols].bitcast(FP8X4),
                    lhsT_scale=w2_scales[:, cols],
                    rhs=hidden_codes(g, lo, hi),
                    rhs_scale=joint_scales[:, :CHUNK] if (g, lo) == (1, CHUNK) else h_scales[g][:, toks],
                    start=(g == 0),
                    stop=(g == 1),
                )
            return bank

        def copy_out(lo, hi, bank):
            y[lo // CHUNK] = sb([P, CHUNK], F32, "y_%d" % (lo // CHUNK))
            nc.scalar.copy(out=y[lo // CHUNK][:], in_=bank[:])

        def weigh(lo, hi, bank):
            y[lo // CHUNK] = sb([P, CHUNK], F32, "y_%d" % (lo // CHUNK))
            nc.vector.tensor_tensor(out=y[lo // CHUNK][:], in0=bank[:], in1=gates[:, lo:hi], op=MULT)

        def scatter_on_scalar(lo, hi):
            nc.scalar.activation(out=result[:].indirect(entries(lo, hi)), in_=y[lo // CHUNK][:], func=COPY)

        def scatter(lo, hi):
            nc.vector.tensor_tensor(result[:].indirect(entries(lo, hi)), y[lo // CHUNK][:], gates[:, lo:hi], MULT)

        def gather_words(c):
            lo, hi = cuts[c], cuts[c + 1]
            nc.vector.tensor_copy(x_codes[:, lo:hi], word_window[:, : reach[c]].indirect(entries(lo, hi)))

        nc.vector.tensor_copy(x_bytes[:], scale_window[:].bitcast(U8).indirect(offsets[:]))
        cast(nc.scalar.copy, "w1", 0, 0, PACK)
        cast(nc.scalar.copy, "w1", 256, 0, 2)
        cast(nc.scalar.copy, "w1", 256, 2, PACK)
        quantise_weights("w1", 0, 0, 2, grouped["w1", 0][:, :2])
        keep_clock("bank_y", 2, [CHUNK, CHUNK], P)
        cast(nc.vector.tensor_copy, "w3", 0, 0, 2)
        quantise_weights("w1", 0, 2, PACK, grouped["w1", 0][:, 2:])
        keep_clock("bank_y", 2, [PASS, PASS], P // 2)
        cast(nc.scalar.copy, "w3", 0, 2, PACK)
        cast(nc.scalar.copy, "w3", W3_CUT, 2, PACK)
        cast(nc.vector.tensor_copy, "w3", W3_CUT, 0, 2)
        quantise_weights("w3", 0, 0, 2, grouped["w3", 0][:, :2])
        quantise_weights("w3", 0, 2, PACK, grouped["w3", 0][:, 2:])
        for c in range(len(reach)):
            gather_words(c)
        for n in range(2):
            sigmoid_tile(0, n)
        w1_words = sb([P, PACK, P, PACK], BF16, "grouped_w1_1")
        cast_on_gpsimd(w1_words[:], "w1", PASS, 0, PACK, 0, 48)
        cast_on_gpsimd(w1_words[:], "w1", PASS + 192, 0, PACK, 48, P)
        w3_high = sb([P, 2, P, PACK], BF16, "grouped_w3_1_high")
        cast_on_gpsimd(w3_high[:], "w3", PASS, 2, PACK, 0, 64)
        for n in range(8):
            gated_tile(0, n)
            if n + 2 < 8:
                sigmoid_tile(0, n + 2)
        codes["w1", 1] = sb([P, PASS], U32, "codes_w1_1", "sig_0_6")
        quantise_weights("w1", 1, 0, 2, w1_words[:, :2])
        quantise_weights("w1", 1, 2, PACK, w1_words[:, 2:])
        w3_low = sb([P, 2, P, PACK], BF16, "grouped_w3_1_low", "sig_0_4")
        cast_on_scalar(w3_low[:], "w3", PASS, 0, 2, 0, 64)
        cast_on_scalar(w3_low[:], "w3", PASS + 256, 0, 2, 64, P)
        quantise_hidden(0, 0, 256, "sig_0_7")
        cast_on_scalar(w3_high[:], "w3", PASS + 256, 2, PACK, 64, P)
        quantise_weights("w3", 1, 0, 2, w3_low[:])
        quantise_weights("w3", 1, 2, 3, w3_high[:, :1])
        quantise_weights("w3", 1, 3, 4, w3_high[:, 1:])
        keep_clock("bank_w3_0", 1, [PASS], P // 2)
        keep_clock("bank_w3_1", 1, [PASS], P // 2)
        sigmoid_tile(1, 0)
        sigmoid_tile(1, 2)
        quantise_hidden(0, 256, 768, "raw_w3_768")
        cast_w2()
        for n, ahead in ((0, 3), (2, 1), (3, 5), (1, 4)):
            gated_tile(1, n)
            sigmoid_tile(1, ahead)
        linear = linear_tile(5)
        sigmoid_tile(1, 6)
        sigmoid_tile(1, 7)
        quantise_joint()
        quantise_hidden(1, 0, 256)
        gated_tile_on_gpsimd(5, linear)
        upper = second_layer(256, 512)
        lower = second_layer(0, 256)
        gated_tile(1, 4)
        weigh(256, 512, upper)
        scatter_on_scalar(256, 512)
        gated_tile(1, 6)
        weigh(0, 256, lower)
        scatter_on_scalar(0, 256)
        gated_tile(1, 7)
        quantise_hidden(1, 512, 768)
        copy_out(512, 768, second_layer(512, 768))
        quantise_hidden(0, 768, S, "linear")
        quantise_hidden(1, 768, S, "sig_1_7")
        copy_out(768, S, second_layer(768, S))
        settled = sb([P, 2 * CHUNK], F32, "settled", "hidden_0_256")
        nc.vector.tensor_copy(out=settled[:], in_=result[:, : 2 * CHUNK])
        nc.sync.dma_start(out=out[:, : 2 * CHUNK], in_=settled[:])
        scatter(512, 768)
        scatter(768, S)
        nc.sync.dma_start(out=out[:, 2 * CHUNK :], in_=result[:, 2 * CHUNK :])
